import numpy as np
import ml_dtypes


def mxq(x, axis, fmt="e4m3"):
    dtype, down = {"e4m3": (ml_dtypes.float8_e4m3fn, 7), "e5m2": (ml_dtypes.float8_e5m2, 14)}[fmt]
    v = np.moveaxis(np.asarray(x, np.float32).astype(ml_dtypes.bfloat16).astype(np.float64), axis, -1)
    blocks = v.reshape(v.shape[:-1] + (-1, 32))
    amax = np.abs(blocks).max(-1, keepdims=True)
    byte = np.maximum(np.where(amax > 0, np.frexp(amax)[1] - 1 + 127, 0) - down, 1)
    scale = np.exp2(byte - 127.0)
    codes = (blocks / scale).astype(np.float32).astype(dtype).astype(np.float64)
    return np.moveaxis((codes * scale).reshape(v.shape), -1, axis)


WIDE = False


def mx_kscale(k):
    if not WIDE:
        return np.ones(k)
    levels = np.array([30, -30])
    if k % 512:
        return np.exp2(np.random.permutation(np.resize(levels, k // 32))).repeat(32)
    a = np.empty((k // 512, 16))
    for p in range(k // 512):
        a[p, :8] = np.random.permutation(np.resize(levels, 8))
        for g in range(8):
            far = levels[np.abs(levels - a[p, g]) >= 10]
            a[p, g + 8] = far[np.random.randint(len(far))]
    return np.exp2(a.ravel()).repeat(32)


BF16 = ml_dtypes.bfloat16


def bf(x):
    return np.asarray(x, np.float32).astype(BF16)


def f64(x):
    return np.asarray(x).astype(np.float64)


E2M1 = np.array([0.0, 0.5, 1.0, 1.5, 2.0, 3.0, 4.0, 6.0, -0.0, -0.5, -1.0, -1.5, -2.0, -3.0, -4.0, -6.0])


def pack_weight(w, fmt):
    k, n = w.shape
    w = f64(bf(w)).reshape(k // 32, 32, n)
    amax = np.abs(w).max(1)
    if fmt in ("e4m3", "e5m2"):
        byte = np.frexp(amax)[1] - 1 + 127 - (7 if fmt == "e4m3" else 14)
    else:
        mant, ex = np.frexp(amax / 6.0)
        byte = np.where(mant > 0.5, ex, ex - 1) + 127
    byte = np.clip(np.where(amax > 0, byte, 1), 1, 254)
    scaled = (w * np.exp2(127.0 - byte)[:, None, :]).reshape(k, n).astype(np.float32)
    by_word = np.ascontiguousarray(scaled.reshape(k // 512, 128, 4, n).transpose(0, 1, 3, 2))
    if fmt in ("e4m3", "e5m2"):
        words = by_word.astype(ml_dtypes.float8_e4m3fn if fmt == "e4m3" else ml_dtypes.float8_e5m2).view(np.uint8)
    else:
        c = by_word.astype(ml_dtypes.float4_e2m1fn).view(np.uint8) & 0xF
        words = c[..., 0::2] | (c[..., 1::2] << 4)
    return np.ascontiguousarray(words), np.ascontiguousarray(byte.astype(np.uint8).reshape(k // 512, 16, n))


def unpack_weight(words, scales, fmt):
    g, p, n, _ = words.shape
    if fmt in ("e4m3", "e5m2"):
        vals = np.ascontiguousarray(words).view(ml_dtypes.float8_e4m3fn if fmt == "e4m3" else ml_dtypes.float8_e5m2).astype(np.float64)
    else:
        nib = np.empty((g, p, n, 4), np.uint8)
        nib[..., 0::2] = words & 0xF
        nib[..., 1::2] = words >> 4
        vals = E2M1[nib]
    vals = vals * np.repeat(np.exp2(scales.astype(np.float64) - 127.0), 8, axis=1)[..., None]
    return vals.transpose(0, 1, 3, 2).reshape(g * 512, n)


H, D, N = 1536, 1024, 1024


def setup_inputs():
    s = mx_kscale(H)
    r = mx_kscale(D)
    G = np.random.standard_normal((H, N)) * np.exp(0.5 * np.random.standard_normal((H, N)))
    g_words, g_scales = pack_weight(G * s[:, None], "e5m2")
    w = np.random.standard_normal((H, H)) / np.sqrt(H)
    u = np.random.standard_normal((H, D)) / np.sqrt(D)
    low = np.random.standard_normal((D, N))
    h = np.tanh(0.7 * np.random.standard_normal(H))
    return {"g_words": g_words,
            "g_scales": g_scales,
            "w": bf(w / s),
            "u": bf(u / r),
            "low": bf(low * r[:, None]),
            "h": bf(h)}


def reference(g_words, g_scales, w, u, low, h):
    G = unpack_weight(g_words, g_scales, "e5m2")
    carried = mxq(f64(w), 1, "e4m3") @ G
    below = mxq(f64(u), 1, "e4m3") @ mxq(f64(low), 0, "e4m3")
    slope = 1.0 - np.square(f64(h))
    return slope[:, None] * (carried + below)

@@ -1,0 +1,454 @@
+from contextlib import ExitStack
+
+import concourse.mybir as mybir
+from concourse.masks import make_identity
+
+H, D, N = 1536, 1024, 1024
+FLOPS = 2 * H * N * (H + D)
+
+F32 = mybir.dt.float32
+BF16 = mybir.dt.bfloat16
+I32 = mybir.dt.int32
+U32 = mybir.dt.uint32
+U8 = mybir.dt.uint8
+E4M3 = mybir.dt.float8_e4m3fn_x4
+E5M2 = mybir.dt.float8_e5m2_x4
+COPY = mybir.ActivationFunctionType.Copy
+MULT = mybir.AluOpType.mult
+
+P = 128
+K_PASS = 512
+HALF = 512
+TILES = H // P
+W_PASSES = H // K_PASS
+U_PASSES = D // K_PASS
+PASSES = W_PASSES + U_PASSES
+PAIRS = K_PASS // 2
+
+LOADS = [('w', 0), ('w', 1), ('w', 2), ('u', 0), ('u', 1), ('u', 2), ('gs', 0), ('g', 0), ('low', 0, 0), ('low', 1, 0), ('w', 3), ('u', 3), ('gs', 1), ('g', 1), ('low', 0, 1), ('w', 4), ('u', 4), ('low', 1, 1), ('w', 5), ('u', 5), ('w', 6), ('u', 6), ('w', 7), ('u', 7), ('w', 8), ('u', 8), ('w', 9), ('u', 9), ('w', 10), ('u', 10), ('w', 11), ('u', 11)]
+STEPS = [
+    ('split', 0, 0, 3, 'v'),
+    ('split', 1, 0, 3, 'v'),
+    ('split', 2, 0, 3, 'v'),
+    ('turn', ((0, 0), (0, 1)), 0),
+    ('turn', ((0, 2), (1, 0)), 0),
+    ('turn', ((1, 1), (1, 2)), 0),
+    ('turn', ((2, 0), (2, 1)), 0),
+    ('empty', (0, 0), 's'),
+    ('empty', (0, 2), 's'),
+    ('split', 0, 3, 5, 'v'),
+    ('quant', (0, 0)),
+    ('split', 1, 3, 5, 'v'),
+    ('quant', (0, 2)),
+    ('split', 2, 3, 5, 'v'),
+    ('turn', ((2, 2), (0, 3)), 0),
+    ('turn', ((0, 4), (1, 3)), 0),
+    ('turn', ((1, 4), (2, 3)), 0),
+    ('turn', ((2, 4),), 0),
+    ('empty', (1, 1), 's'),
+    ('empty', (2, 0), 's'),
+    ('empty', (2, 2), 's'),
+    ('quant', (1, 1)),
+    ('quant', (2, 0)),
+    ('quant', (2, 2)),
+    ('empty', (0, 4), 's'),
+    ('empty', (1, 4), 'v'),
+    ('empty', (2, 4), 's'),
+    ('quant', (0, 4)),
+    ('quant', (1, 4)),
+    ('quant', (2, 4)),
+    ('mm', 0, 0, 0, 0),
+    ('mm', 0, 0, 1, 0),
+    ('mm', 0, 0, 2, 0),
+    ('mm', 1, 0, 0, 0),
+    ('mm', 1, 0, 1, 0),
+    ('mm', 1, 0, 2, 0),
+    ('mm', 2, 0, 0, 0),
+    ('mm', 2, 0, 1, 0),
+    ('mm', 2, 0, 2, 0),
+    ('weave', 0, 0, 0, 256, 'v'),
+    ('weave', 0, 0, 256, 512, 's'),
+    ('lowq', 0, 0),
+    ('weave', 1, 0, 0, 256, 'v'),
+    ('weave', 1, 0, 256, 512, 's'),
+    ('lowq', 1, 0),
+    ('split', 3, 0, 3, 'v'),
+    ('split', 3, 3, 5, 'v'),
+    ('mm', 0, 0, 3, 0),
+    ('mm', 1, 0, 3, 0),
+    ('mm', 2, 0, 3, 0),
+    ('mm', 0, 0, 4, 0),
+    ('out', 0, 0, 's', 1),
+    ('mm', 1, 0, 4, 0),
+    ('out', 1, 0, 's', 1),
+    ('mm', 2, 0, 4, 0),
+    ('out', 2, 0, 's', 1),
+    ('turn', ((3, 0), (3, 1)), 0),
+    ('turn', ((3, 2), (3, 3)), 0),
+    ('turn', ((3, 4),), 0),
+    ('empty', (3, 0), 'v'),
+    ('empty', (3, 2), 's'),
+    ('empty', (3, 4), 'v'),
+    ('quant', (3, 0)),
+    ('quant', (3, 2)),
+    ('quant', (3, 4)),
+    ('mm', 0, 1, 0, 0),
+    ('mm', 0, 1, 1, 0),
+    ('mm', 0, 1, 2, 0),
+    ('mm', 1, 1, 0, 0),
+    ('mm', 1, 1, 1, 0),
+    ('mm', 1, 1, 2, 0),
+    ('mm', 2, 1, 0, 0),
+    ('mm', 2, 1, 1, 0),
+    ('mm', 2, 1, 2, 0),
+    ('weave', 0, 1, 0, 256, 'v'),
+    ('weave', 0, 1, 256, 512, 's'),
+    ('lowq', 0, 1),
+    ('split', 4, 0, 3, 'v'),
+    ('split', 4, 3, 5, 'v'),
+    ('weave', 1, 1, 0, 256, 'v'),
+    ('weave', 1, 1, 256, 512, 's'),
+    ('lowq', 1, 1),
+    ('mm', 3, 0, 0, 0),
+    ('mm', 3, 0, 1, 0),
+    ('mm', 3, 0, 2, 0),
+    ('mm', 3, 0, 3, 0),
+    ('mm', 3, 0, 4, 0),
+    ('out', 3, 0, 's', 1),
+    ('mm', 3, 1, 0, 0),
+    ('mm', 3, 1, 1, 0),
+    ('mm', 3, 1, 2, 0),
+    ('turn', ((4, 0), (4, 1)), 0),
+    ('turn', ((4, 2), (4, 3)), 0),
+    ('turn', ((4, 4),), 0),
+    ('empty', (4, 0), 's'),
+    ('empty', (4, 2), 's'),
+    ('empty', (4, 4), 'v'),
+    ('quant', (4, 0)),
+    ('quant', (4, 2)),
+    ('quant', (4, 4)),
+    ('split', 5, 0, 3, 'v'),
+    ('split', 5, 3, 5, 'v'),
+    ('split', 6, 0, 3, 'v'),
+    ('split', 6, 3, 5, 'v'),
+    ('mm', 0, 1, 3, 0),
+    ('mm', 1, 1, 3, 0),
+    ('mm', 2, 1, 3, 0),
+    ('mm', 3, 1, 3, 0),
+    ('mm', 0, 1, 4, 0),
+    ('out', 0, 1, 's', 1),
+    ('mm', 1, 1, 4, 0),
+    ('out', 1, 1, 's', 1),
+    ('mm', 2, 1, 4, 0),
+    ('out', 2, 1, 's', 1),
+    ('mm', 3, 1, 4, 0),
+    ('out', 3, 1, 'v', 1),
+    ('turn', ((5, 0), (5, 1)), 0),
+    ('turn', ((5, 2), (5, 3)), 0),
+    ('turn', ((5, 4), (6, 0)), 0),
+    ('turn', ((6, 1), (6, 2)), 0),
+    ('turn', ((6, 3), (6, 4)), 0),
+    ('split', 7, 0, 3, 'v'),
+    ('split', 7, 3, 5, 'v'),
+    ('split', 8, 0, 3, 'v'),
+    ('split', 8, 3, 5, 'v'),
+    ('empty', (5, 0), 's'),
+    ('empty', (5, 2), 's'),
+    ('empty', (5, 4), 's'),
+    ('empty', (6, 1), 's'),
+    ('empty', (6, 3), 's'),
+    ('quant', (5, 0)),
+    ('quant', (5, 2)),
+    ('quant', (5, 4)),
+    ('quant', (6, 1)),
+    ('quant', (6, 3)),
+    ('mm', 4, 0, 0, 0),
+    ('mm', 4, 0, 1, 0),
+    ('mm', 4, 0, 2, 0),
+    ('mm', 4, 0, 3, 0),
+    ('mm', 4, 0, 4, 0),
+    ('out', 4, 0, 's', 1),
+    ('mm', 4, 1, 0, 0),
+    ('mm', 4, 1, 1, 0),
+    ('mm', 4, 1, 2, 0),
+    ('mm', 4, 1, 3, 0),
+    ('mm', 4, 1, 4, 0),
+    ('out', 4, 1, 's', 1),
+    ('turn', ((7, 0), (7, 1)), 0),
+    ('turn', ((7, 2), (7, 3)), 0),
+    ('turn', ((7, 4), (8, 0)), 0),
+    ('turn', ((8, 1), (8, 2)), 0),
+    ('turn', ((8, 3), (8, 4)), 0),
+    ('split', 9, 0, 3, 'v'),
+    ('split', 9, 3, 5, 'v'),
+    ('split', 10, 0, 3, 'v'),
+    ('split', 10, 3, 5, 'v'),
+    ('empty', (7, 0), 's'),
+    ('empty', (7, 2), 's'),
+    ('empty', (7, 4), 's'),
+    ('empty', (8, 1), 's'),
+    ('empty', (8, 3), 's'),
+    ('quant', (7, 0)),
+    ('quant', (7, 2)),
+    ('quant', (7, 4)),
+    ('quant', (8, 1)),
+    ('quant', (8, 3)),
+    ('mm', 5, 0, 0, 0),
+    ('mm', 5, 0, 1, 0),
+    ('mm', 5, 0, 2, 0),
+    ('mm', 5, 0, 3, 0),
+    ('mm', 5, 0, 4, 0),
+    ('out', 5, 0, 's', 1),
+    ('mm', 5, 1, 0, 0),
+    ('mm', 5, 1, 1, 0),
+    ('mm', 5, 1, 2, 0),
+    ('mm', 5, 1, 3, 0),
+    ('mm', 5, 1, 4, 0),
+    ('out', 5, 1, 's', 1),
+    ('mm', 6, 0, 0, 0),
+    ('mm', 6, 0, 1, 0),
+    ('mm', 6, 0, 2, 0),
+    ('mm', 6, 0, 3, 0),
+    ('mm', 6, 0, 4, 0),
+    ('out', 6, 0, 's', 1),
+    ('mm', 6, 1, 0, 0),
+    ('mm', 6, 1, 1, 0),
+    ('mm', 6, 1, 2, 0),
+    ('mm', 6, 1, 3, 0),
+    ('mm', 6, 1, 4, 0),
+    ('out', 6, 1, 's', 1),
+    ('turn', ((9, 0), (9, 1)), 0),
+    ('turn', ((9, 2), (9, 3)), 0),
+    ('turn', ((9, 4), (10, 0)), 0),
+    ('turn', ((10, 1), (10, 2)), 0),
+    ('turn', ((10, 3), (10, 4)), 0),
+    ('split', 11, 0, 3, 'v'),
+    ('split', 11, 3, 5, 'v'),
+    ('empty', (9, 0), 's'),
+    ('empty', (9, 2), 's'),
+    ('empty', (9, 4), 's'),
+    ('empty', (10, 1), 's'),
+    ('empty', (10, 3), 's'),
+    ('quant', (9, 0)),
+    ('quant', (9, 2)),
+    ('quant', (9, 4)),
+    ('quant', (10, 1)),
+    ('quant', (10, 3)),
+    ('mm', 7, 0, 0, 0),
+    ('mm', 7, 0, 1, 0),
+    ('mm', 7, 0, 2, 0),
+    ('mm', 7, 0, 3, 0),
+    ('mm', 7, 0, 4, 0),
+    ('out', 7, 0, 's', 1),
+    ('mm', 7, 1, 0, 0),
+    ('mm', 7, 1, 1, 0),
+    ('mm', 7, 1, 2, 0),
+    ('mm', 7, 1, 3, 0),
+    ('mm', 7, 1, 4, 0),
+    ('out', 7, 1, 's', 1),
+    ('mm', 8, 0, 0, 0),
+    ('mm', 8, 0, 1, 0),
+    ('mm', 8, 0, 2, 0),
+    ('mm', 8, 0, 3, 0),
+    ('mm', 8, 0, 4, 0),
+    ('out', 8, 0, 's', 1),
+    ('mm', 8, 1, 0, 0),
+    ('mm', 8, 1, 1, 0),
+    ('mm', 8, 1, 2, 0),
+    ('mm', 8, 1, 3, 0),
+    ('mm', 8, 1, 4, 0),
+    ('out', 8, 1, 's', 1),
+    ('turn', ((11, 0), (11, 1)), 0),
+    ('turn', ((11, 2), (11, 3)), 0),
+    ('turn', ((11, 4),), 0),
+    ('empty', (11, 0), 's'),
+    ('empty', (11, 2), 's'),
+    ('empty', (11, 4), 's'),
+    ('quant', (11, 0)),
+    ('quant', (11, 2)),
+    ('quant', (11, 4)),
+    ('mm', 9, 0, 0, 0),
+    ('mm', 9, 0, 1, 0),
+    ('mm', 9, 0, 2, 0),
+    ('mm', 9, 0, 3, 0),
+    ('mm', 9, 0, 4, 0),
+    ('out', 9, 0, 's', 1),
+    ('mm', 9, 1, 0, 0),
+    ('mm', 9, 1, 1, 0),
+    ('mm', 9, 1, 2, 0),
+    ('mm', 9, 1, 3, 0),
+    ('mm', 9, 1, 4, 0),
+    ('out', 9, 1, 's', 1),
+    ('mm', 10, 0, 0, 0),
+    ('mm', 10, 0, 1, 0),
+    ('mm', 10, 0, 2, 0),
+    ('mm', 10, 0, 3, 0),
+    ('mm', 10, 0, 4, 0),
+    ('out', 10, 0, 's', 1),
+    ('mm', 10, 1, 0, 0),
+    ('mm', 10, 1, 1, 0),
+    ('mm', 10, 1, 2, 0),
+    ('mm', 10, 1, 3, 0),
+    ('mm', 10, 1, 4, 0),
+    ('out', 10, 1, 's', 1),
+    ('mm', 11, 0, 0, 0),
+    ('mm', 11, 0, 1, 0),
+    ('mm', 11, 0, 2, 0),
+    ('mm', 11, 0, 3, 0),
+    ('mm', 11, 0, 4, 0),
+    ('out', 11, 0, 's', 1),
+    ('mm', 11, 1, 0, 0),
+    ('mm', 11, 1, 1, 0),
+    ('mm', 11, 1, 2, 0),
+    ('mm', 11, 1, 3, 0),
+    ('mm', 11, 1, 4, 0),
+    ('out', 11, 1, 's', 2),
+]
+
+
+def tile_stacked_rtrl_step_e4_kernel(tc, g_words, g_scales, w, u, low, h, out):
+    nc = tc.nc
+    w_rows = w.rearrange("(p i) k -> p i k", i=TILES)
+    u_rows = u.rearrange("(p i) k -> p i k", i=TILES)
+    out_rows = out.rearrange("(p i) n -> p i n", i=TILES)
+    g_bytes = g_words.rearrange("g p n t -> p g (n t)")
+    g_scale_rows = g_scales.rearrange("g q n -> q g n")
+
+    with ExitStack() as ctx:
+        keep = ctx.enter_context(tc.tile_pool(name="keep", bufs=1))
+        work = ctx.enter_context(tc.tile_pool(name="work", bufs=4))
+        psum = ctx.enter_context(tc.psum_pool(name="psum", bufs=4))
+        ctx.enter_context(tc.manual_schedule())
+
+        ident = keep.tile([P, P], F32, name="ident")
+        make_identity(nc, ident[:])
+
+        h_sb = keep.tile([P, TILES], BF16, name="h_sb")
+        nc.scalar.dma_start(out=h_sb[:], in_=h.rearrange("(p i) -> p i", i=TILES))
+
+        g_plane = [keep.tile([P, W_PASSES, HALF], U8, name="g_plane%d" % hf, align_bytes=64) for hf in range(2)]
+        for hf in range(2):
+            nc.vector.memset(g_plane[hf][:].bitcast(I32), 0)
+        g_codes = [keep.tile([P, W_PASSES, HALF], U32, name="g_codes%d" % hf, align_bytes=64) for hf in range(2)]
+        rows = [keep.tile([P, H + D], BF16, name="rows%d" % i, align_bytes=64) for i in range(TILES)]
+        low_raw, low_grouped, low_codes, low_plane = {}, {}, {}, {}
+
+        for item in LOADS:
+            if item[0] == "w":
+                nc.sync.dma_start(out=rows[item[1]][:, 0:H], in_=w_rows[:, item[1], :])
+            elif item[0] == "u":
+                nc.sync.dma_start(out=rows[item[1]][:, H:H + D], in_=u_rows[:, item[1], :])
+            elif item[0] == "gs":
+                hf = item[1]
+                for q in range(4):
+                    nc.sync.dma_start(out=g_plane[hf][32 * q:32 * q + 4, :, :].bitcast(I32),
+                                      in_=g_scale_rows[4 * q:4 * q + 4, :, hf * HALF:(hf + 1) * HALF].bitcast(I32))
+            elif item[0] == "g":
+                hf = item[1]
+                nc.sync.dma_start(out=g_codes[hf][:].bitcast(I32), in_=g_bytes[:, :, 4 * hf * HALF:4 * (hf + 1) * HALF].bitcast(I32))
+            else:
+                c, hf = item[1], item[2]
+                low_raw[c, hf] = keep.tile([P, 4, HALF], BF16, name="low_raw%d%d" % (c, hf), align_bytes=64)
+                nc.sync.dma_start(out=low_raw[c, hf][:],
+                                  in_=low[c * K_PASS:(c + 1) * K_PASS, hf * HALF:(hf + 1) * HALF].rearrange("(p t) n -> p t n", t=4))
+
+        h_squared = keep.tile([P, TILES], F32, name="h_squared")
+        slope = keep.tile([P, TILES], F32, name="slope")
+        nc.vector.tensor_tensor(out=h_squared[:], in0=h_sb[:], in1=h_sb[:], op=MULT)
+        nc.scalar.activation(out=slope[:], in_=h_squared[:], func=COPY, bias=1.0, scale=-1.0)
+
+        free_banks = list(range(8))
+        held, done_passes = {}, {}
+
+        def take_bank(key, shape):
+            held[key] = free_banks.pop(0)
+            return psum.tile(shape, F32, name="bank%d" % held[key], tag="bank%d" % held[key], bufs=1)
+
+        sources, banks, groups, codes, planes, sums = {}, {}, {}, {}, {}, {}
+
+        def copy_on(engine, dst, src):
+            if engine == "v":
+                nc.vector.tensor_copy(out=dst, in_=src)
+            else:
+                nc.scalar.copy(out=dst, in_=src)
+
+        def pairs_of(i, c0, c1):
+            return rows[i][:].bitcast(F32)[:, c0 * PAIRS:c1 * PAIRS].rearrange("p (j e) -> p e j", e=2)
+
+        for step in STEPS:
+            kind = step[0]
+            if kind == "weave":
+                c, hf, n0, n1, engine = step[1:]
+                if (c, hf) not in low_grouped:
+                    low_grouped[c, hf] = work.tile([P, HALF, 4], BF16, name="low_grouped", tag="low_grouped", bufs=2, align_bytes=64)
+                copy_on(engine, low_grouped[c, hf][:, n0:n1, :].rearrange("p (a b) t -> p a t b", b=4),
+                        low_raw[c, hf][:, :, n0:n1].rearrange("p t (a b) -> p a t b", b=4))
+            elif kind == "lowq":
+                c, hf = step[1:]
+                low_codes[c, hf] = keep.tile([P, HALF], U32, name="low_codes%d%d" % (c, hf), align_bytes=64)
+                low_plane[c, hf] = keep.tile([P, HALF], U8, name="low_plane%d%d" % (c, hf), align_bytes=64)
+                nc.vector.quantize_mx(out=low_codes[c, hf][:].bitcast(E4M3), scales=low_plane[c, hf][:],
+                                      in_=low_grouped[c, hf][:].rearrange("p n t -> p (n t)"))
+            elif kind == "split":
+                i, c0, c1, engine = step[1:]
+                if engine == "n":
+                    continue
+                split = work.tile([P, 2, (c1 - c0) * P], F32, name="split", tag="split", bufs=6)
+                copy_on(engine, split[:], pairs_of(i, c0, c1))
+                for c in range(c0, c1):
+                    sources[i, c] = split[:, :, (c - c0) * P:(c - c0 + 1) * P]
+            elif kind == "turn":
+                units = step[1]
+                bank = take_bank(("turned", units[0]), [P, len(units), 2, P])
+                for s, (i, c) in enumerate(units):
+                    source = sources[i, c] if (i, c) in sources else pairs_of(i, c, c + 1)
+                    for e in range(2):
+                        nc.tensor.transpose(out=bank[:, s, e, :], in_=source[:, e, :], identity=ident[:])
+                banks[units[0]] = (units, bank)
+            elif kind == "empty":
+                first, engine = step[1:]
+                units, bank = banks[first]
+                free_banks.append(held["turned", first])
+                groups[first] = work.tile([P, len(units) * K_PASS], BF16, name="grouped", tag="grouped", bufs=6, align_bytes=64)
+                copy_on(engine, groups[first][:].bitcast(F32).rearrange("p (s m e) -> p s m e", m=P, e=2),
+                        bank[:].rearrange("p s e m -> p s m e"))
+            elif kind == "quant":
+                first = step[1]
+                units = banks[first][0]
+                unit_codes = keep.tile([P, len(units) * P], U32, name="codes%d_%d" % first, align_bytes=64)
+                unit_plane = keep.tile([P, len(units) * P], U8, name="plane%d_%d" % first, align_bytes=64)
+                nc.vector.quantize_mx(out=unit_codes[:].bitcast(E4M3), scales=unit_plane[:], in_=groups[first][:])
+                for s, unit in enumerate(units):
+                    codes[unit] = unit_codes[:, s * P:(s + 1) * P]
+                    planes[unit] = unit_plane[:, s * P:(s + 1) * P]
+                if first == (0, 0):
+                    warm_codes, warm_plane = unit_codes, unit_plane
+            elif kind == "warm":
+                scratch = take_bank("warm", [P, 2 * P])
+                free_banks.append(held["warm"])
+                for repeat in range(step[1]):
+                    nc.tensor.matmul_mx(out=scratch[:], lhsT=codes[0, 0].bitcast(E4M3), lhsT_scale=planes[0, 0],
+                                        rhs=warm_codes[:].bitcast(E4M3), rhs_scale=warm_plane[:], start=True, stop=True)
+            elif kind == "mm":
+                i, hf, c = step[1:4]
+                before = done_passes.get((i, hf), 0)
+                done_passes[i, hf] = before + 1
+                if before == 0:
+                    sums[i, hf] = take_bank(("sums", i, hf), [P, HALF])
+                if c < W_PASSES:
+                    moving, moving_plane = g_codes[hf][:, c, :].bitcast(E5M2), g_plane[hf][:, c, :]
+                else:
+                    moving, moving_plane = low_codes[c - W_PASSES, hf][:].bitcast(E4M3), low_plane[c - W_PASSES, hf][:]
+                nc.tensor.matmul_mx(out=sums[i, hf][:], lhsT=codes[i, c].bitcast(E4M3), lhsT_scale=planes[i, c],
+                                    rhs=moving, rhs_scale=moving_plane, start=(before == 0), stop=(before == PASSES - 1))
+            else:
+                i, hf, engine, pieces = step[1:]
+                free_banks.append(held["sums", i, hf])
+                result = work.tile([P, HALF], F32, name="result", tag="result", bufs=12)
+                for n0 in range(0, HALF, HALF // pieces):
+                    cols = slice(n0, n0 + HALF // pieces)
+                    if engine == "v":
+                        nc.vector.tensor_scalar(out=result[:, cols], in0=sums[i, hf][:, cols], scalar1=slope[:, i:i + 1], scalar2=None, op0=MULT)
+                    else:
+                        nc.scalar.activation(out=result[:, cols], in_=sums[i, hf][:, cols], func=COPY, scale=slope[:, i:i + 1])
+                    nc.sync.dma_start(out=out_rows[:, i, hf * HALF + n0:hf * HALF + n0 + HALF // pieces], in_=result[:, cols])

@@ -14,6 +14,7 @@ U8 = mybir.dt.uint8
 E4M3 = mybir.dt.float8_e4m3fn_x4
 E5M2 = mybir.dt.float8_e5m2_x4
 COPY = mybir.ActivationFunctionType.Copy
+SQUARE = mybir.ActivationFunctionType.Square
 MULT = mybir.AluOpType.mult
 
 P = 128
@@ -25,7 +26,7 @@ U_PASSES = D // K_PASS
 PASSES = W_PASSES + U_PASSES
 PAIRS = K_PASS // 2
 
-LOADS = [('w', 0), ('w', 1), ('w', 2), ('u', 0), ('u', 1), ('u', 2), ('gs', 0), ('g', 0), ('low', 0, 0), ('low', 1, 0), ('w', 3), ('u', 3), ('gs', 1), ('g', 1), ('low', 0, 1), ('w', 4), ('u', 4), ('low', 1, 1), ('w', 5), ('u', 5), ('w', 6), ('u', 6), ('w', 7), ('u', 7), ('w', 8), ('u', 8), ('w', 9), ('u', 9), ('w', 10), ('u', 10), ('w', 11), ('u', 11)]
+LOADS = [('w', 0), ('w', 1), ('w', 2), ('u', 0), ('u', 1), ('u', 2), ('gs', 0), ('g', 0, 0), ('low', 0, 0), ('g', 0, 1), ('low', 1, 0), ('g', 0, 2), ('w', 3), ('u', 3), ('gs', 1), ('g', 1, 0), ('g', 1, 1), ('low', 0, 1), ('g', 1, 2), ('w', 4), ('low', 1, 1), ('u', 4), ('w', 5), ('u', 5), ('w', 6), ('u', 6), ('wq', 7), ('u', 7), ('wq', 8), ('u', 8), ('wq', 9), ('u', 9), ('wq', 10), ('u', 10), ('wq', 11), ('u', 11)]
 STEPS = [
     ('split', 0, 0, 3, 'v'),
     ('split', 1, 0, 3, 'v'),
@@ -35,6 +36,7 @@ STEPS = [
     ('turn', ((1, 1), (1, 2)), 0),
     ('turn', ((2, 0), (2, 1)), 0),
     ('empty', (0, 0), 's'),
+    ('slope_rows',),
     ('empty', (0, 2), 's'),
     ('split', 0, 3, 5, 'v'),
     ('quant', (0, 0)),
@@ -45,6 +47,7 @@ STEPS = [
     ('turn', ((0, 4), (1, 3)), 0),
     ('turn', ((1, 4), (2, 3)), 0),
     ('turn', ((2, 4),), 0),
+    ('slope_turn',),
     ('empty', (1, 1), 's'),
     ('empty', (2, 0), 's'),
     ('empty', (2, 2), 's'),
@@ -52,63 +55,56 @@ STEPS = [
     ('quant', (2, 0)),
     ('quant', (2, 2)),
     ('empty', (0, 4), 's'),
+    ('slope_out',),
     ('empty', (1, 4), 'v'),
+    ('weave', 0, 0, 0, 256, 'v'),
+    ('weave', 0, 0, 256, 512, 's'),
     ('empty', (2, 4), 's'),
     ('quant', (0, 4)),
     ('quant', (1, 4)),
+    ('lowq', 0, 0),
     ('quant', (2, 4)),
     ('mm', 0, 0, 0, 0),
-    ('mm', 0, 0, 1, 0),
-    ('mm', 0, 0, 2, 0),
     ('mm', 1, 0, 0, 0),
-    ('mm', 1, 0, 1, 0),
-    ('mm', 1, 0, 2, 0),
     ('mm', 2, 0, 0, 0),
+    ('mm', 0, 0, 1, 0),
+    ('mm', 1, 0, 1, 0),
     ('mm', 2, 0, 1, 0),
-    ('mm', 2, 0, 2, 0),
-    ('weave', 0, 0, 0, 256, 'v'),
-    ('weave', 0, 0, 256, 512, 's'),
-    ('lowq', 0, 0),
     ('weave', 1, 0, 0, 256, 'v'),
     ('weave', 1, 0, 256, 512, 's'),
     ('lowq', 1, 0),
-    ('split', 3, 0, 3, 'v'),
-    ('split', 3, 3, 5, 'v'),
     ('mm', 0, 0, 3, 0),
     ('mm', 1, 0, 3, 0),
     ('mm', 2, 0, 3, 0),
+    ('mm', 0, 0, 2, 0),
+    ('mm', 1, 0, 2, 0),
+    ('mm', 2, 0, 2, 0),
+    ('split', 3, 0, 3, 's'),
+    ('split', 3, 3, 5, 'v'),
     ('mm', 0, 0, 4, 0),
-    ('out', 0, 0, 's', 1),
+    ('out', 0, 0, 'v', 1),
     ('mm', 1, 0, 4, 0),
-    ('out', 1, 0, 's', 1),
     ('mm', 2, 0, 4, 0),
-    ('out', 2, 0, 's', 1),
     ('turn', ((3, 0), (3, 1)), 0),
     ('turn', ((3, 2), (3, 3)), 0),
     ('turn', ((3, 4),), 0),
+    ('out', 1, 0, 's', 1),
     ('empty', (3, 0), 'v'),
     ('empty', (3, 2), 's'),
     ('empty', (3, 4), 'v'),
     ('quant', (3, 0)),
     ('quant', (3, 2)),
     ('quant', (3, 4)),
+    ('out', 2, 0, 's', 1),
     ('mm', 0, 1, 0, 0),
-    ('mm', 0, 1, 1, 0),
-    ('mm', 0, 1, 2, 0),
     ('mm', 1, 1, 0, 0),
-    ('mm', 1, 1, 1, 0),
-    ('mm', 1, 1, 2, 0),
     ('mm', 2, 1, 0, 0),
+    ('mm', 0, 1, 1, 0),
+    ('mm', 1, 1, 1, 0),
     ('mm', 2, 1, 1, 0),
-    ('mm', 2, 1, 2, 0),
     ('weave', 0, 1, 0, 256, 'v'),
     ('weave', 0, 1, 256, 512, 's'),
     ('lowq', 0, 1),
-    ('split', 4, 0, 3, 'v'),
-    ('split', 4, 3, 5, 'v'),
-    ('weave', 1, 1, 0, 256, 'v'),
-    ('weave', 1, 1, 256, 512, 's'),
-    ('lowq', 1, 1),
     ('mm', 3, 0, 0, 0),
     ('mm', 3, 0, 1, 0),
     ('mm', 3, 0, 2, 0),
@@ -117,7 +113,19 @@ STEPS = [
     ('out', 3, 0, 's', 1),
     ('mm', 3, 1, 0, 0),
     ('mm', 3, 1, 1, 0),
+    ('mm', 0, 1, 2, 0),
+    ('mm', 1, 1, 2, 0),
+    ('mm', 2, 1, 2, 0),
     ('mm', 3, 1, 2, 0),
+    ('split', 4, 0, 3, 'v'),
+    ('weave', 1, 1, 0, 256, 'v'),
+    ('weave', 1, 1, 256, 512, 's'),
+    ('split', 4, 3, 5, 'v'),
+    ('lowq', 1, 1),
+    ('mm', 0, 1, 3, 0),
+    ('mm', 1, 1, 3, 0),
+    ('mm', 2, 1, 3, 0),
+    ('mm', 3, 1, 3, 0),
     ('turn', ((4, 0), (4, 1)), 0),
     ('turn', ((4, 2), (4, 3)), 0),
     ('turn', ((4, 4),), 0),
@@ -127,14 +135,6 @@ STEPS = [
     ('quant', (4, 0)),
     ('quant', (4, 2)),
     ('quant', (4, 4)),
-    ('split', 5, 0, 3, 'v'),
-    ('split', 5, 3, 5, 'v'),
-    ('split', 6, 0, 3, 'v'),
-    ('split', 6, 3, 5, 'v'),
-    ('mm', 0, 1, 3, 0),
-    ('mm', 1, 1, 3, 0),
-    ('mm', 2, 1, 3, 0),
-    ('mm', 3, 1, 3, 0),
     ('mm', 0, 1, 4, 0),
     ('out', 0, 1, 's', 1),
     ('mm', 1, 1, 4, 0),
@@ -143,15 +143,21 @@ STEPS = [
     ('out', 2, 1, 's', 1),
     ('mm', 3, 1, 4, 0),
     ('out', 3, 1, 'v', 1),
+    ('split', 5, 0, 3, 'v'),
+    ('split', 5, 3, 5, 'v'),
+    ('split', 6, 0, 3, 'v'),
+    ('split', 6, 3, 5, 'v'),
+    ('mm', 4, 0, 0, 0),
+    ('mm', 4, 0, 1, 0),
+    ('mm', 4, 0, 2, 0),
+    ('mm', 4, 0, 3, 0),
+    ('mm', 4, 0, 4, 0),
+    ('out', 4, 0, 's', 0),
     ('turn', ((5, 0), (5, 1)), 0),
     ('turn', ((5, 2), (5, 3)), 0),
     ('turn', ((5, 4), (6, 0)), 0),
     ('turn', ((6, 1), (6, 2)), 0),
     ('turn', ((6, 3), (6, 4)), 0),
-    ('split', 7, 0, 3, 'v'),
-    ('split', 7, 3, 5, 'v'),
-    ('split', 8, 0, 3, 'v'),
-    ('split', 8, 3, 5, 'v'),
     ('empty', (5, 0), 's'),
     ('empty', (5, 2), 's'),
     ('empty', (5, 4), 's'),
@@ -162,123 +168,128 @@ STEPS = [
     ('quant', (5, 4)),
     ('quant', (6, 1)),
     ('quant', (6, 3)),
-    ('mm', 4, 0, 0, 0),
-    ('mm', 4, 0, 1, 0),
-    ('mm', 4, 0, 2, 0),
-    ('mm', 4, 0, 3, 0),
-    ('mm', 4, 0, 4, 0),
-    ('out', 4, 0, 's', 1),
     ('mm', 4, 1, 0, 0),
     ('mm', 4, 1, 1, 0),
     ('mm', 4, 1, 2, 0),
     ('mm', 4, 1, 3, 0),
     ('mm', 4, 1, 4, 0),
-    ('out', 4, 1, 's', 1),
-    ('turn', ((7, 0), (7, 1)), 0),
-    ('turn', ((7, 2), (7, 3)), 0),
-    ('turn', ((7, 4), (8, 0)), 0),
-    ('turn', ((8, 1), (8, 2)), 0),
-    ('turn', ((8, 3), (8, 4)), 0),
-    ('split', 9, 0, 3, 'v'),
-    ('split', 9, 3, 5, 'v'),
-    ('split', 10, 0, 3, 'v'),
-    ('split', 10, 3, 5, 'v'),
-    ('empty', (7, 0), 's'),
-    ('empty', (7, 2), 's'),
-    ('empty', (7, 4), 's'),
-    ('empty', (8, 1), 's'),
-    ('empty', (8, 3), 's'),
-    ('quant', (7, 0)),
-    ('quant', (7, 2)),
-    ('quant', (7, 4)),
-    ('quant', (8, 1)),
-    ('quant', (8, 3)),
+    ('out', 4, 1, 's', 0),
+    ('store', 4),
+    ('split', 7, 0, 3, 'v'),
+    ('dvt', 7),
+    ('split', 7, 3, 5, 'v'),
+    ('split', 8, 3, 5, 'v'),
     ('mm', 5, 0, 0, 0),
     ('mm', 5, 0, 1, 0),
     ('mm', 5, 0, 2, 0),
     ('mm', 5, 0, 3, 0),
     ('mm', 5, 0, 4, 0),
-    ('out', 5, 0, 's', 1),
+    ('out', 5, 0, 's', 0),
+    ('ilv', 7, 0, 's'),
+    ('ilv', 7, 1, 'v'),
     ('mm', 5, 1, 0, 0),
     ('mm', 5, 1, 1, 0),
     ('mm', 5, 1, 2, 0),
     ('mm', 5, 1, 3, 0),
     ('mm', 5, 1, 4, 0),
-    ('out', 5, 1, 's', 1),
+    ('out', 5, 1, 's', 0),
+    ('store', 5),
+    ('turn', ((7, 3), (7, 4)), 0),
+    ('turn', ((8, 3), (8, 4)), 0),
+    ('split', 8, 0, 3, 'v'),
+    ('quant', (7, 0)),
+    ('quant', (7, 2)),
+    ('dvt', 8),
+    ('empty', (7, 3), 's'),
+    ('empty', (8, 3), 's'),
+    ('quant', (7, 3)),
+    ('quant', (8, 3)),
     ('mm', 6, 0, 0, 0),
     ('mm', 6, 0, 1, 0),
     ('mm', 6, 0, 2, 0),
     ('mm', 6, 0, 3, 0),
     ('mm', 6, 0, 4, 0),
-    ('out', 6, 0, 's', 1),
+    ('out', 6, 0, 's', 0),
+    ('ilv', 8, 0, 's'),
+    ('ilv', 8, 1, 'v'),
     ('mm', 6, 1, 0, 0),
     ('mm', 6, 1, 1, 0),
     ('mm', 6, 1, 2, 0),
     ('mm', 6, 1, 3, 0),
     ('mm', 6, 1, 4, 0),
-    ('out', 6, 1, 's', 1),
-    ('turn', ((9, 0), (9, 1)), 0),
-    ('turn', ((9, 2), (9, 3)), 0),
-    ('turn', ((9, 4), (10, 0)), 0),
-    ('turn', ((10, 1), (10, 2)), 0),
-    ('turn', ((10, 3), (10, 4)), 0),
-    ('split', 11, 0, 3, 'v'),
+    ('out', 6, 1, 's', 0),
+    ('store', 6),
+    ('split', 9, 0, 3, 'v'),
+    ('quant', (8, 0)),
+    ('quant', (8, 2)),
+    ('dvt', 9),
+    ('split', 9, 3, 5, 'v'),
+    ('split', 10, 3, 5, 'v'),
     ('split', 11, 3, 5, 'v'),
-    ('empty', (9, 0), 's'),
-    ('empty', (9, 2), 's'),
-    ('empty', (9, 4), 's'),
-    ('empty', (10, 1), 's'),
-    ('empty', (10, 3), 's'),
-    ('quant', (9, 0)),
-    ('quant', (9, 2)),
-    ('quant', (9, 4)),
-    ('quant', (10, 1)),
-    ('quant', (10, 3)),
     ('mm', 7, 0, 0, 0),
     ('mm', 7, 0, 1, 0),
     ('mm', 7, 0, 2, 0),
     ('mm', 7, 0, 3, 0),
     ('mm', 7, 0, 4, 0),
-    ('out', 7, 0, 's', 1),
+    ('out', 7, 0, 's', 0),
+    ('ilv', 9, 0, 's'),
+    ('ilv', 9, 1, 'v'),
     ('mm', 7, 1, 0, 0),
     ('mm', 7, 1, 1, 0),
     ('mm', 7, 1, 2, 0),
     ('mm', 7, 1, 3, 0),
     ('mm', 7, 1, 4, 0),
-    ('out', 7, 1, 's', 1),
+    ('out', 7, 1, 's', 0),
+    ('store', 7),
+    ('turn', ((9, 3), (9, 4)), 0),
+    ('turn', ((10, 3), (10, 4)), 0),
+    ('turn', ((11, 3), (11, 4)), 0),
+    ('split', 10, 0, 3, 'v'),
+    ('quant', (9, 0)),
+    ('quant', (9, 2)),
+    ('dvt', 10),
+    ('empty', (9, 3), 's'),
+    ('empty', (10, 3), 's'),
+    ('empty', (11, 3), 's'),
+    ('quant', (9, 3)),
+    ('quant', (10, 3)),
+    ('quant', (11, 3)),
     ('mm', 8, 0, 0, 0),
     ('mm', 8, 0, 1, 0),
     ('mm', 8, 0, 2, 0),
     ('mm', 8, 0, 3, 0),
     ('mm', 8, 0, 4, 0),
-    ('out', 8, 0, 's', 1),
+    ('out', 8, 0, 's', 0),
+    ('ilv', 10, 0, 's'),
+    ('ilv', 10, 1, 'v'),
     ('mm', 8, 1, 0, 0),
     ('mm', 8, 1, 1, 0),
     ('mm', 8, 1, 2, 0),
     ('mm', 8, 1, 3, 0),
     ('mm', 8, 1, 4, 0),
-    ('out', 8, 1, 's', 1),
-    ('turn', ((11, 0), (11, 1)), 0),
-    ('turn', ((11, 2), (11, 3)), 0),
-    ('turn', ((11, 4),), 0),
-    ('empty', (11, 0), 's'),
-    ('empty', (11, 2), 's'),
-    ('empty', (11, 4), 's'),
-    ('quant', (11, 0)),
-    ('quant', (11, 2)),
-    ('quant', (11, 4)),
+    ('out', 8, 1, 's', 0),
+    ('store', 8),
+    ('split', 11, 0, 3, 'v'),
+    ('quant', (10, 0)),
+    ('quant', (10, 2)),
+    ('dvt', 11),
     ('mm', 9, 0, 0, 0),
     ('mm', 9, 0, 1, 0),
     ('mm', 9, 0, 2, 0),
     ('mm', 9, 0, 3, 0),
     ('mm', 9, 0, 4, 0),
-    ('out', 9, 0, 's', 1),
+    ('out', 9, 0, 's', 0),
+    ('ilv', 11, 0, 's'),
+    ('ilv', 11, 1, 'v'),
     ('mm', 9, 1, 0, 0),
     ('mm', 9, 1, 1, 0),
     ('mm', 9, 1, 2, 0),
     ('mm', 9, 1, 3, 0),
     ('mm', 9, 1, 4, 0),
-    ('out', 9, 1, 's', 1),
+    ('out', 9, 1, 's', 0),
+    ('store', 9),
+    ('quant', (11, 0)),
+    ('quant', (11, 2)),
     ('mm', 10, 0, 0, 0),
     ('mm', 10, 0, 1, 0),
     ('mm', 10, 0, 2, 0),
@@ -308,9 +319,10 @@ STEPS = [
 
 def tile_stacked_rtrl_step_e4_kernel(tc, g_words, g_scales, w, u, low, h, out):
     nc = tc.nc
-    w_rows = w.rearrange("(p i) k -> p i k", i=TILES)
-    u_rows = u.rearrange("(p i) k -> p i k", i=TILES)
-    out_rows = out.rearrange("(p i) n -> p i n", i=TILES)
+    w_rows = w.rearrange("(i p) k -> p i k", p=P)
+    u_rows = u.rearrange("(i p) k -> p i k", p=P)
+    out_rows = out.rearrange("(i p) n -> p i n", p=P)
+    w_quarters = w.rearrange("m k -> (m k)").rearrange("(i r y q x) -> i q r y x", i=TILES, r=32, q=4, x=P)
     g_bytes = g_words.rearrange("g p n t -> p g (n t)")
     g_scale_rows = g_scales.rearrange("g q n -> q g n")
 
@@ -323,8 +335,12 @@ def tile_stacked_rtrl_step_e4_kernel(tc, g_words, g_scales, w, u, low, h, out):
         ident = keep.tile([P, P], F32, name="ident")
         make_identity(nc, ident[:])
 
-        h_sb = keep.tile([P, TILES], BF16, name="h_sb")
-        nc.scalar.dma_start(out=h_sb[:], in_=h.rearrange("(p i) -> p i", i=TILES))
+        h_sb = keep.tile([TILES, P], BF16, name="h_sb")
+        h_rows = h.rearrange("(i p) -> i p", p=P)
+        nc.scalar.dma_start(out=h_sb[0:8, :], in_=h_rows[0:8, :])
+        nc.scalar.dma_start(out=h_sb[8:TILES, :], in_=h_rows[8:TILES, :])
+        slope_rows = keep.tile([P, P], F32, name="slope_rows")
+        nc.scalar.activation(out=slope_rows[:], in_=ident[:], func=COPY, bias=0.0, scale=0.0)
 
         g_plane = [keep.tile([P, W_PASSES, HALF], U8, name="g_plane%d" % hf, align_bytes=64) for hf in range(2)]
         for hf in range(2):
@@ -336,6 +352,10 @@ def tile_stacked_rtrl_step_e4_kernel(tc, g_words, g_scales, w, u, low, h, out):
         for item in LOADS:
             if item[0] == "w":
                 nc.sync.dma_start(out=rows[item[1]][:, 0:H], in_=w_rows[:, item[1], :])
+            elif item[0] == "wq":
+                for q in (0, 2, 1, 3):
+                    nc.sync.dma_start(out=rows[item[1]][32 * q:32 * q + 32, 0:H].rearrange("r (y x) -> r y x", x=P),
+                                      in_=w_quarters[item[1], q])
             elif item[0] == "u":
                 nc.sync.dma_start(out=rows[item[1]][:, H:H + D], in_=u_rows[:, item[1], :])
             elif item[0] == "gs":
@@ -344,21 +364,19 @@ def tile_stacked_rtrl_step_e4_kernel(tc, g_words, g_scales, w, u, low, h, out):
                     nc.sync.dma_start(out=g_plane[hf][32 * q:32 * q + 4, :, :].bitcast(I32),
                                       in_=g_scale_rows[4 * q:4 * q + 4, :, hf * HALF:(hf + 1) * HALF].bitcast(I32))
             elif item[0] == "g":
-                hf = item[1]
-                nc.sync.dma_start(out=g_codes[hf][:].bitcast(I32), in_=g_bytes[:, :, 4 * hf * HALF:4 * (hf + 1) * HALF].bitcast(I32))
+                hf, c = item[1], item[2]
+                nc.sync.dma_start(out=g_codes[hf][:, c, :].bitcast(I32), in_=g_bytes[:, c, 4 * hf * HALF:4 * (hf + 1) * HALF].bitcast(I32))
             else:
                 c, hf = item[1], item[2]
                 low_raw[c, hf] = keep.tile([P, 4, HALF], BF16, name="low_raw%d%d" % (c, hf), align_bytes=64)
                 nc.sync.dma_start(out=low_raw[c, hf][:],
                                   in_=low[c * K_PASS:(c + 1) * K_PASS, hf * HALF:(hf + 1) * HALF].rearrange("(p t) n -> p t n", t=4))
 
-        h_squared = keep.tile([P, TILES], F32, name="h_squared")
+        h_squared = keep.tile([TILES, P], F32, name="h_squared")
         slope = keep.tile([P, TILES], F32, name="slope")
-        nc.vector.tensor_tensor(out=h_squared[:], in0=h_sb[:], in1=h_sb[:], op=MULT)
-        nc.scalar.activation(out=slope[:], in_=h_squared[:], func=COPY, bias=1.0, scale=-1.0)
 
         free_banks = list(range(8))
-        held, done_passes = {}, {}
+        held, done_passes, blocks, flipped, whole = {}, {}, {}, {}, {}
 
         def take_bank(key, shape):
             held[key] = free_banks.pop(0)
@@ -393,10 +411,39 @@ def tile_stacked_rtrl_step_e4_kernel(tc, g_words, g_scales, w, u, low, h, out):
                 i, c0, c1, engine = step[1:]
                 if engine == "n":
                     continue
-                split = work.tile([P, 2, (c1 - c0) * P], F32, name="split", tag="split", bufs=6)
+                split = work.tile([P, 2, (c1 - c0) * P], F32, name="split", tag="split", bufs=6, align_bytes=64)
+                if ("wq", i) in LOADS and c0 == 0:
+                    copy_on(engine, split[:].rearrange("p e (b x) -> p (e b x)", b=4).rearrange("p (b e x) -> p b e x", b=4, e=2),
+                            rows[i][:].bitcast(F32)[:, 0:H // 2].rearrange("p (b x e) -> p b e x", b=4, e=2))
+                    blocks[i] = split
+                    continue
                 copy_on(engine, split[:], pairs_of(i, c0, c1))
                 for c in range(c0, c1):
                     sources[i, c] = split[:, :, (c - c0) * P:(c - c0 + 1) * P]
+            elif kind == "slope_rows":
+                nc.scalar.activation(out=h_squared[:], in_=h_sb[:], func=SQUARE)
+                nc.scalar.activation(out=slope_rows[0:TILES, :], in_=h_squared[:], func=COPY, bias=1.0, scale=-1.0)
+            elif kind == "slope_turn":
+                slope_bank = take_bank("slope", [P, P])
+                nc.tensor.transpose(out=slope_bank[:], in_=slope_rows[:], identity=ident[:])
+            elif kind == "slope_out":
+                free_banks.append(held["slope"])
+                nc.scalar.copy(out=slope[:], in_=slope_bank[:, 0:TILES])
+            elif kind == "dvt":
+                i = step[1]
+                flipped[i] = work.tile([P, H // 2], F32, name="flipped", tag="flipped", bufs=2, align_bytes=64)
+                nc.vector.transpose(out=flipped[i][:], in_=blocks[i][:].rearrange("p e x -> p (e x)"))
+            elif kind == "ilv":
+                i, part, engine = step[1:]
+                units = ((i, 0), (i, 1)) if part == 0 else ((i, 2),)
+                banks[units[0]] = (units, None)
+                groups[units[0]] = work.tile([P, len(units) * K_PASS], BF16, name="grouped", tag="grouped", bufs=6, align_bytes=64)
+                dst = groups[units[0]][:].bitcast(F32).rearrange("p (c r a y) -> p a c r y", r=32, a=2, y=4)
+                src = flipped[i][:].rearrange("p (a y c r) -> p a c r y", a=2, y=4, r=32)
+                for a in range(2):
+                    copy_on(engine, dst[:, a], src[:, a, units[0][1]:units[-1][1] + 1])
+            elif kind == "store":
+                nc.sync.dma_start(out=out_rows[:, step[1], :], in_=whole[step[1]][:])
             elif kind == "turn":
                 units = step[1]
                 bank = take_bank(("turned", units[0]), [P, len(units), 2, P])
@@ -444,11 +491,16 @@ def tile_stacked_rtrl_step_e4_kernel(tc, g_words, g_scales, w, u, low, h, out):
             else:
                 i, hf, engine, pieces = step[1:]
                 free_banks.append(held["sums", i, hf])
-                result = work.tile([P, HALF], F32, name="result", tag="result", bufs=12)
+                if i not in whole:
+                    whole[i] = keep.tile([P, N], F32, name="result%d" % i)
+                result = whole[i][:, hf * HALF:(hf + 1) * HALF]
+                store_now = pieces > 0
+                pieces = max(pieces, 1)
                 for n0 in range(0, HALF, HALF // pieces):
                     cols = slice(n0, n0 + HALF // pieces)
                     if engine == "v":
                         nc.vector.tensor_scalar(out=result[:, cols], in0=sums[i, hf][:, cols], scalar1=slope[:, i:i + 1], scalar2=None, op0=MULT)
                     else:
                         nc.scalar.activation(out=result[:, cols], in_=sums[i, hf][:, cols], func=COPY, scale=slope[:, i:i + 1])
-                    nc.sync.dma_start(out=out_rows[:, i, hf * HALF + n0:hf * HALF + n0 + HALF // pieces], in_=result[:, cols])
+                    if store_now:
+                        nc.sync.dma_start(out=out_rows[:, i, hf * HALF + n0:hf * HALF + n0 + HALF // pieces], in_=result[:, cols])

@@ -26,17 +26,17 @@ U_PASSES = D // K_PASS
 PASSES = W_PASSES + U_PASSES
 PAIRS = K_PASS // 2
 
-LOADS = [('w', 0), ('w', 1), ('w', 2), ('u', 0), ('u', 1), ('u', 2), ('gs', 0), ('g', 0, 0), ('low', 0, 0), ('g', 0, 1), ('low', 1, 0), ('g', 0, 2), ('w', 3), ('u', 3), ('gs', 1), ('g', 1, 0), ('g', 1, 1), ('low', 0, 1), ('g', 1, 2), ('w', 4), ('low', 1, 1), ('u', 4), ('w', 5), ('u', 5), ('w', 6), ('u', 6), ('wq', 7), ('u', 7), ('wq', 8), ('u', 8), ('wq', 9), ('u', 9), ('wq', 10), ('u', 10), ('wq', 11), ('u', 11)]
+LOADS = [('w', 0), ('w', 1), ('w', 2), ('u', 0), ('u', 1), ('u', 2), ('low', 0, 0), ('gs', 0), ('g', 0, 0), ('g', 0, 1), ('low', 1, 0), ('g', 0, 2), ('gs', 1), ('g', 1, 0), ('w', 3), ('u', 3), ('g', 1, 1), ('g', 1, 2), ('low', 0, 1), ('w', 4), ('low', 1, 1), ('u', 4), ('w', 5), ('u', 5), ('w', 6), ('u', 6), ('w', 7), ('u', 7), ('wq', 8), ('u', 8), ('u', 9), ('u', 10), ('u', 11), ('wq', 9), ('wq', 10), ('wq', 11)]
 STEPS = [
     ('split', 0, 0, 3, 'v'),
     ('split', 1, 0, 3, 'v'),
+    ('slope_rows',),
     ('split', 2, 0, 3, 'v'),
     ('turn', ((0, 0), (0, 1)), 0),
     ('turn', ((0, 2), (1, 0)), 0),
     ('turn', ((1, 1), (1, 2)), 0),
     ('turn', ((2, 0), (2, 1)), 0),
     ('empty', (0, 0), 's'),
-    ('slope_rows',),
     ('empty', (0, 2), 's'),
     ('split', 0, 3, 5, 'v'),
     ('quant', (0, 0)),
@@ -53,17 +53,16 @@ STEPS = [
     ('empty', (2, 2), 's'),
     ('quant', (1, 1)),
     ('quant', (2, 0)),
-    ('quant', (2, 2)),
-    ('empty', (0, 4), 's'),
-    ('slope_out',),
-    ('empty', (1, 4), 'v'),
     ('weave', 0, 0, 0, 256, 'v'),
     ('weave', 0, 0, 256, 512, 's'),
+    ('quant', (2, 2)),
+    ('empty', (0, 4), 's'),
+    ('empty', (1, 4), 'v'),
+    ('lowq', 0, 0),
+    ('slope_out',),
     ('empty', (2, 4), 's'),
     ('quant', (0, 4)),
     ('quant', (1, 4)),
-    ('lowq', 0, 0),
-    ('quant', (2, 4)),
     ('mm', 0, 0, 0, 0),
     ('mm', 1, 0, 0, 0),
     ('mm', 2, 0, 0, 0),
@@ -72,6 +71,7 @@ STEPS = [
     ('mm', 2, 0, 1, 0),
     ('weave', 1, 0, 0, 256, 'v'),
     ('weave', 1, 0, 256, 512, 's'),
+    ('quant', (2, 4)),
     ('lowq', 1, 0),
     ('mm', 0, 0, 3, 0),
     ('mm', 1, 0, 3, 0),
@@ -79,47 +79,47 @@ STEPS = [
     ('mm', 0, 0, 2, 0),
     ('mm', 1, 0, 2, 0),
     ('mm', 2, 0, 2, 0),
-    ('split', 3, 0, 3, 's'),
+    ('mm', 0, 1, 0, 0),
+    ('mm', 1, 1, 0, 0),
+    ('mm', 2, 1, 0, 0),
+    ('split', 3, 0, 3, 'v'),
     ('split', 3, 3, 5, 'v'),
     ('mm', 0, 0, 4, 0),
-    ('out', 0, 0, 'v', 1),
+    ('out', 0, 0, 's', 0),
     ('mm', 1, 0, 4, 0),
+    ('out', 1, 0, 's', 0),
     ('mm', 2, 0, 4, 0),
     ('turn', ((3, 0), (3, 1)), 0),
     ('turn', ((3, 2), (3, 3)), 0),
     ('turn', ((3, 4),), 0),
-    ('out', 1, 0, 's', 1),
     ('empty', (3, 0), 'v'),
     ('empty', (3, 2), 's'),
     ('empty', (3, 4), 'v'),
     ('quant', (3, 0)),
     ('quant', (3, 2)),
     ('quant', (3, 4)),
-    ('out', 2, 0, 's', 1),
-    ('mm', 0, 1, 0, 0),
-    ('mm', 1, 1, 0, 0),
-    ('mm', 2, 1, 0, 0),
+    ('out', 2, 0, 's', 0),
     ('mm', 0, 1, 1, 0),
     ('mm', 1, 1, 1, 0),
     ('mm', 2, 1, 1, 0),
+    ('mm', 0, 1, 2, 0),
+    ('mm', 1, 1, 2, 0),
+    ('mm', 2, 1, 2, 0),
     ('weave', 0, 1, 0, 256, 'v'),
     ('weave', 0, 1, 256, 512, 's'),
+    ('split', 4, 0, 3, 'v'),
     ('lowq', 0, 1),
     ('mm', 3, 0, 0, 0),
     ('mm', 3, 0, 1, 0),
     ('mm', 3, 0, 2, 0),
     ('mm', 3, 0, 3, 0),
     ('mm', 3, 0, 4, 0),
-    ('out', 3, 0, 's', 1),
     ('mm', 3, 1, 0, 0),
     ('mm', 3, 1, 1, 0),
-    ('mm', 0, 1, 2, 0),
-    ('mm', 1, 1, 2, 0),
-    ('mm', 2, 1, 2, 0),
     ('mm', 3, 1, 2, 0),
-    ('split', 4, 0, 3, 'v'),
     ('weave', 1, 1, 0, 256, 'v'),
     ('weave', 1, 1, 256, 512, 's'),
+    ('out', 3, 0, 's', 0),
     ('split', 4, 3, 5, 'v'),
     ('lowq', 1, 1),
     ('mm', 0, 1, 3, 0),
@@ -136,17 +136,23 @@ STEPS = [
     ('quant', (4, 2)),
     ('quant', (4, 4)),
     ('mm', 0, 1, 4, 0),
-    ('out', 0, 1, 's', 1),
+    ('out', 0, 1, 's', 0),
+    ('store', 0),
     ('mm', 1, 1, 4, 0),
-    ('out', 1, 1, 's', 1),
+    ('out', 1, 1, 's', 0),
+    ('store', 1),
     ('mm', 2, 1, 4, 0),
-    ('out', 2, 1, 's', 1),
+    ('out', 2, 1, 's', 0),
+    ('store', 2),
     ('mm', 3, 1, 4, 0),
-    ('out', 3, 1, 'v', 1),
     ('split', 5, 0, 3, 'v'),
+    ('out', 3, 1, 's', 0),
+    ('store', 3),
     ('split', 5, 3, 5, 'v'),
     ('split', 6, 0, 3, 'v'),
     ('split', 6, 3, 5, 'v'),
+    ('split', 7, 0, 3, 'v'),
+    ('split', 7, 3, 5, 'v'),
     ('mm', 4, 0, 0, 0),
     ('mm', 4, 0, 1, 0),
     ('mm', 4, 0, 2, 0),
@@ -158,16 +164,25 @@ STEPS = [
     ('turn', ((5, 4), (6, 0)), 0),
     ('turn', ((6, 1), (6, 2)), 0),
     ('turn', ((6, 3), (6, 4)), 0),
+    ('turn', ((7, 0), (7, 1)), 0),
+    ('turn', ((7, 2), (7, 3)), 0),
+    ('turn', ((7, 4),), 0),
     ('empty', (5, 0), 's'),
     ('empty', (5, 2), 's'),
-    ('empty', (5, 4), 's'),
+    ('empty', (5, 4), 'v'),
     ('empty', (6, 1), 's'),
     ('empty', (6, 3), 's'),
+    ('empty', (7, 0), 'v'),
+    ('empty', (7, 2), 's'),
+    ('empty', (7, 4), 's'),
     ('quant', (5, 0)),
     ('quant', (5, 2)),
     ('quant', (5, 4)),
     ('quant', (6, 1)),
     ('quant', (6, 3)),
+    ('quant', (7, 0)),
+    ('quant', (7, 2)),
+    ('quant', (7, 4)),
     ('mm', 4, 1, 0, 0),
     ('mm', 4, 1, 1, 0),
     ('mm', 4, 1, 2, 0),
@@ -175,18 +190,12 @@ STEPS = [
     ('mm', 4, 1, 4, 0),
     ('out', 4, 1, 's', 0),
     ('store', 4),
-    ('split', 7, 0, 3, 'v'),
-    ('dvt', 7),
-    ('split', 7, 3, 5, 'v'),
-    ('split', 8, 3, 5, 'v'),
     ('mm', 5, 0, 0, 0),
     ('mm', 5, 0, 1, 0),
     ('mm', 5, 0, 2, 0),
     ('mm', 5, 0, 3, 0),
     ('mm', 5, 0, 4, 0),
     ('out', 5, 0, 's', 0),
-    ('ilv', 7, 0, 's'),
-    ('ilv', 7, 1, 'v'),
     ('mm', 5, 1, 0, 0),
     ('mm', 5, 1, 1, 0),
     ('mm', 5, 1, 2, 0),
@@ -194,16 +203,12 @@ STEPS = [
     ('mm', 5, 1, 4, 0),
     ('out', 5, 1, 's', 0),
     ('store', 5),
-    ('turn', ((7, 3), (7, 4)), 0),
-    ('turn', ((8, 3), (8, 4)), 0),
     ('split', 8, 0, 3, 'v'),
-    ('quant', (7, 0)),
-    ('quant', (7, 2)),
     ('dvt', 8),
-    ('empty', (7, 3), 's'),
-    ('empty', (8, 3), 's'),
-    ('quant', (7, 3)),
-    ('quant', (8, 3)),
+    ('split', 8, 3, 5, 'v'),
+    ('split', 9, 3, 5, 'v'),
+    ('split', 10, 3, 5, 'v'),
+    ('split', 11, 3, 5, 'v'),
     ('mm', 6, 0, 0, 0),
     ('mm', 6, 0, 1, 0),
     ('mm', 6, 0, 2, 0),
@@ -219,13 +224,22 @@ STEPS = [
     ('mm', 6, 1, 4, 0),
     ('out', 6, 1, 's', 0),
     ('store', 6),
+    ('turn', ((8, 3), (8, 4)), 0),
+    ('turn', ((9, 3), (9, 4)), 0),
+    ('turn', ((10, 3), (10, 4)), 0),
+    ('turn', ((11, 3), (11, 4)), 0),
     ('split', 9, 0, 3, 'v'),
     ('quant', (8, 0)),
     ('quant', (8, 2)),
     ('dvt', 9),
-    ('split', 9, 3, 5, 'v'),
-    ('split', 10, 3, 5, 'v'),
-    ('split', 11, 3, 5, 'v'),
+    ('empty', (8, 3), 's'),
+    ('empty', (9, 3), 's'),
+    ('empty', (10, 3), 's'),
+    ('empty', (11, 3), 's'),
+    ('quant', (8, 3)),
+    ('quant', (9, 3)),
+    ('quant', (10, 3)),
+    ('quant', (11, 3)),
     ('mm', 7, 0, 0, 0),
     ('mm', 7, 0, 1, 0),
     ('mm', 7, 0, 2, 0),
@@ -241,19 +255,10 @@ STEPS = [
     ('mm', 7, 1, 4, 0),
     ('out', 7, 1, 's', 0),
     ('store', 7),
-    ('turn', ((9, 3), (9, 4)), 0),
-    ('turn', ((10, 3), (10, 4)), 0),
-    ('turn', ((11, 3), (11, 4)), 0),
     ('split', 10, 0, 3, 'v'),
     ('quant', (9, 0)),
     ('quant', (9, 2)),
     ('dvt', 10),
-    ('empty', (9, 3), 's'),
-    ('empty', (10, 3), 's'),
-    ('empty', (11, 3), 's'),
-    ('quant', (9, 3)),
-    ('quant', (10, 3)),
-    ('quant', (11, 3)),
     ('mm', 8, 0, 0, 0),
     ('mm', 8, 0, 1, 0),
     ('mm', 8, 0, 2, 0),

@@ -15,311 +15,37 @@ E4M3 = mybir.dt.float8_e4m3fn_x4
 E5M2 = mybir.dt.float8_e5m2_x4
 COPY = mybir.ActivationFunctionType.Copy
 SQUARE = mybir.ActivationFunctionType.Square
-MULT = mybir.AluOpType.mult
 
 P = 128
-K_PASS = 512
+QUAD = 32
+QUADS = P // QUAD
+PACK = 4
+K_PASS = P * PACK
+PAIRS = K_PASS // 2
 HALF = 512
 TILES = H // P
 W_PASSES = H // K_PASS
-U_PASSES = D // K_PASS
-PASSES = W_PASSES + U_PASSES
-PAIRS = K_PASS // 2
+PASSES = W_PASSES + D // K_PASS
+BANKS = 8
+SLABS_PER_BANK = 2
+MX_ALIGN = 256
 
-LOADS = [('w', 0), ('w', 1), ('w', 2), ('u', 0), ('u', 1), ('u', 2), ('low', 0, 0), ('gs', 0), ('g', 0, 0), ('g', 0, 1), ('low', 1, 0), ('g', 0, 2), ('gs', 1), ('g', 1, 0), ('w', 3), ('u', 3), ('g', 1, 1), ('g', 1, 2), ('low', 0, 1), ('w', 4), ('low', 1, 1), ('u', 4), ('w', 5), ('u', 5), ('w', 6), ('u', 6), ('w', 7), ('u', 7), ('wq', 8), ('u', 8), ('u', 9), ('u', 10), ('u', 11), ('wq', 9), ('wq', 10), ('wq', 11)]
-STEPS = [
-    ('split', 0, 0, 3, 'v'),
-    ('split', 1, 0, 3, 'v'),
-    ('slope_rows',),
-    ('split', 2, 0, 3, 'v'),
-    ('turn', ((0, 0), (0, 1)), 0),
-    ('turn', ((0, 2), (1, 0)), 0),
-    ('turn', ((1, 1), (1, 2)), 0),
-    ('turn', ((2, 0), (2, 1)), 0),
-    ('empty', (0, 0), 's'),
-    ('empty', (0, 2), 's'),
-    ('split', 0, 3, 5, 'v'),
-    ('quant', (0, 0)),
-    ('split', 1, 3, 5, 'v'),
-    ('quant', (0, 2)),
-    ('split', 2, 3, 5, 'v'),
-    ('turn', ((2, 2), (0, 3)), 0),
-    ('turn', ((0, 4), (1, 3)), 0),
-    ('turn', ((1, 4), (2, 3)), 0),
-    ('turn', ((2, 4),), 0),
-    ('slope_turn',),
-    ('empty', (1, 1), 's'),
-    ('empty', (2, 0), 's'),
-    ('empty', (2, 2), 's'),
-    ('quant', (1, 1)),
-    ('quant', (2, 0)),
-    ('weave', 0, 0, 0, 256, 'v'),
-    ('weave', 0, 0, 256, 512, 's'),
-    ('quant', (2, 2)),
-    ('empty', (0, 4), 's'),
-    ('empty', (1, 4), 'v'),
-    ('lowq', 0, 0),
-    ('slope_out',),
-    ('empty', (2, 4), 's'),
-    ('quant', (0, 4)),
-    ('quant', (1, 4)),
-    ('mm', 0, 0, 0, 0),
-    ('mm', 1, 0, 0, 0),
-    ('mm', 2, 0, 0, 0),
-    ('mm', 0, 0, 1, 0),
-    ('mm', 1, 0, 1, 0),
-    ('mm', 2, 0, 1, 0),
-    ('weave', 1, 0, 0, 256, 'v'),
-    ('weave', 1, 0, 256, 512, 's'),
-    ('quant', (2, 4)),
-    ('lowq', 1, 0),
-    ('mm', 0, 0, 3, 0),
-    ('mm', 1, 0, 3, 0),
-    ('mm', 2, 0, 3, 0),
-    ('mm', 0, 0, 2, 0),
-    ('mm', 1, 0, 2, 0),
-    ('mm', 2, 0, 2, 0),
-    ('mm', 0, 1, 0, 0),
-    ('mm', 1, 1, 0, 0),
-    ('mm', 2, 1, 0, 0),
-    ('split', 3, 0, 3, 'v'),
-    ('split', 3, 3, 5, 'v'),
-    ('mm', 0, 0, 4, 0),
-    ('out', 0, 0, 's', 0),
-    ('mm', 1, 0, 4, 0),
-    ('out', 1, 0, 's', 0),
-    ('mm', 2, 0, 4, 0),
-    ('turn', ((3, 0), (3, 1)), 0),
-    ('turn', ((3, 2), (3, 3)), 0),
-    ('turn', ((3, 4),), 0),
-    ('empty', (3, 0), 'v'),
-    ('empty', (3, 2), 's'),
-    ('empty', (3, 4), 'v'),
-    ('quant', (3, 0)),
-    ('quant', (3, 2)),
-    ('quant', (3, 4)),
-    ('out', 2, 0, 's', 0),
-    ('mm', 0, 1, 1, 0),
-    ('mm', 1, 1, 1, 0),
-    ('mm', 2, 1, 1, 0),
-    ('mm', 0, 1, 2, 0),
-    ('mm', 1, 1, 2, 0),
-    ('mm', 2, 1, 2, 0),
-    ('weave', 0, 1, 0, 256, 'v'),
-    ('weave', 0, 1, 256, 512, 's'),
-    ('split', 4, 0, 3, 'v'),
-    ('lowq', 0, 1),
-    ('mm', 3, 0, 0, 0),
-    ('mm', 3, 0, 1, 0),
-    ('mm', 3, 0, 2, 0),
-    ('mm', 3, 0, 3, 0),
-    ('mm', 3, 0, 4, 0),
-    ('mm', 3, 1, 0, 0),
-    ('mm', 3, 1, 1, 0),
-    ('mm', 3, 1, 2, 0),
-    ('weave', 1, 1, 0, 256, 'v'),
-    ('weave', 1, 1, 256, 512, 's'),
-    ('out', 3, 0, 's', 0),
-    ('split', 4, 3, 5, 'v'),
-    ('lowq', 1, 1),
-    ('mm', 0, 1, 3, 0),
-    ('mm', 1, 1, 3, 0),
-    ('mm', 2, 1, 3, 0),
-    ('mm', 3, 1, 3, 0),
-    ('turn', ((4, 0), (4, 1)), 0),
-    ('turn', ((4, 2), (4, 3)), 0),
-    ('turn', ((4, 4),), 0),
-    ('empty', (4, 0), 's'),
-    ('empty', (4, 2), 's'),
-    ('empty', (4, 4), 'v'),
-    ('quant', (4, 0)),
-    ('quant', (4, 2)),
-    ('quant', (4, 4)),
-    ('mm', 0, 1, 4, 0),
-    ('out', 0, 1, 's', 0),
-    ('store', 0),
-    ('mm', 1, 1, 4, 0),
-    ('out', 1, 1, 's', 0),
-    ('store', 1),
-    ('mm', 2, 1, 4, 0),
-    ('out', 2, 1, 's', 0),
-    ('store', 2),
-    ('mm', 3, 1, 4, 0),
-    ('split', 5, 0, 3, 'v'),
-    ('out', 3, 1, 's', 0),
-    ('store', 3),
-    ('split', 5, 3, 5, 'v'),
-    ('split', 6, 0, 3, 'v'),
-    ('split', 6, 3, 5, 'v'),
-    ('split', 7, 0, 3, 'v'),
-    ('split', 7, 3, 5, 'v'),
-    ('mm', 4, 0, 0, 0),
-    ('mm', 4, 0, 1, 0),
-    ('mm', 4, 0, 2, 0),
-    ('mm', 4, 0, 3, 0),
-    ('mm', 4, 0, 4, 0),
-    ('out', 4, 0, 's', 0),
-    ('turn', ((5, 0), (5, 1)), 0),
-    ('turn', ((5, 2), (5, 3)), 0),
-    ('turn', ((5, 4), (6, 0)), 0),
-    ('turn', ((6, 1), (6, 2)), 0),
-    ('turn', ((6, 3), (6, 4)), 0),
-    ('turn', ((7, 0), (7, 1)), 0),
-    ('turn', ((7, 2), (7, 3)), 0),
-    ('turn', ((7, 4),), 0),
-    ('empty', (5, 0), 's'),
-    ('empty', (5, 2), 's'),
-    ('empty', (5, 4), 'v'),
-    ('empty', (6, 1), 's'),
-    ('empty', (6, 3), 's'),
-    ('empty', (7, 0), 'v'),
-    ('empty', (7, 2), 's'),
-    ('empty', (7, 4), 's'),
-    ('quant', (5, 0)),
-    ('quant', (5, 2)),
-    ('quant', (5, 4)),
-    ('quant', (6, 1)),
-    ('quant', (6, 3)),
-    ('quant', (7, 0)),
-    ('quant', (7, 2)),
-    ('quant', (7, 4)),
-    ('mm', 4, 1, 0, 0),
-    ('mm', 4, 1, 1, 0),
-    ('mm', 4, 1, 2, 0),
-    ('mm', 4, 1, 3, 0),
-    ('mm', 4, 1, 4, 0),
-    ('out', 4, 1, 's', 0),
-    ('store', 4),
-    ('mm', 5, 0, 0, 0),
-    ('mm', 5, 0, 1, 0),
-    ('mm', 5, 0, 2, 0),
-    ('mm', 5, 0, 3, 0),
-    ('mm', 5, 0, 4, 0),
-    ('out', 5, 0, 's', 0),
-    ('mm', 5, 1, 0, 0),
-    ('mm', 5, 1, 1, 0),
-    ('mm', 5, 1, 2, 0),
-    ('mm', 5, 1, 3, 0),
-    ('mm', 5, 1, 4, 0),
-    ('out', 5, 1, 's', 0),
-    ('store', 5),
-    ('split', 8, 0, 3, 'v'),
-    ('dvt', 8),
-    ('split', 8, 3, 5, 'v'),
-    ('split', 9, 3, 5, 'v'),
-    ('split', 10, 3, 5, 'v'),
-    ('split', 11, 3, 5, 'v'),
-    ('mm', 6, 0, 0, 0),
-    ('mm', 6, 0, 1, 0),
-    ('mm', 6, 0, 2, 0),
-    ('mm', 6, 0, 3, 0),
-    ('mm', 6, 0, 4, 0),
-    ('out', 6, 0, 's', 0),
-    ('ilv', 8, 0, 's'),
-    ('ilv', 8, 1, 'v'),
-    ('mm', 6, 1, 0, 0),
-    ('mm', 6, 1, 1, 0),
-    ('mm', 6, 1, 2, 0),
-    ('mm', 6, 1, 3, 0),
-    ('mm', 6, 1, 4, 0),
-    ('out', 6, 1, 's', 0),
-    ('store', 6),
-    ('turn', ((8, 3), (8, 4)), 0),
-    ('turn', ((9, 3), (9, 4)), 0),
-    ('turn', ((10, 3), (10, 4)), 0),
-    ('turn', ((11, 3), (11, 4)), 0),
-    ('split', 9, 0, 3, 'v'),
-    ('quant', (8, 0)),
-    ('quant', (8, 2)),
-    ('dvt', 9),
-    ('empty', (8, 3), 's'),
-    ('empty', (9, 3), 's'),
-    ('empty', (10, 3), 's'),
-    ('empty', (11, 3), 's'),
-    ('quant', (8, 3)),
-    ('quant', (9, 3)),
-    ('quant', (10, 3)),
-    ('quant', (11, 3)),
-    ('mm', 7, 0, 0, 0),
-    ('mm', 7, 0, 1, 0),
-    ('mm', 7, 0, 2, 0),
-    ('mm', 7, 0, 3, 0),
-    ('mm', 7, 0, 4, 0),
-    ('out', 7, 0, 's', 0),
-    ('ilv', 9, 0, 's'),
-    ('ilv', 9, 1, 'v'),
-    ('mm', 7, 1, 0, 0),
-    ('mm', 7, 1, 1, 0),
-    ('mm', 7, 1, 2, 0),
-    ('mm', 7, 1, 3, 0),
-    ('mm', 7, 1, 4, 0),
-    ('out', 7, 1, 's', 0),
-    ('store', 7),
-    ('split', 10, 0, 3, 'v'),
-    ('quant', (9, 0)),
-    ('quant', (9, 2)),
-    ('dvt', 10),
-    ('mm', 8, 0, 0, 0),
-    ('mm', 8, 0, 1, 0),
-    ('mm', 8, 0, 2, 0),
-    ('mm', 8, 0, 3, 0),
-    ('mm', 8, 0, 4, 0),
-    ('out', 8, 0, 's', 0),
-    ('ilv', 10, 0, 's'),
-    ('ilv', 10, 1, 'v'),
-    ('mm', 8, 1, 0, 0),
-    ('mm', 8, 1, 1, 0),
-    ('mm', 8, 1, 2, 0),
-    ('mm', 8, 1, 3, 0),
-    ('mm', 8, 1, 4, 0),
-    ('out', 8, 1, 's', 0),
-    ('store', 8),
-    ('split', 11, 0, 3, 'v'),
-    ('quant', (10, 0)),
-    ('quant', (10, 2)),
-    ('dvt', 11),
-    ('mm', 9, 0, 0, 0),
-    ('mm', 9, 0, 1, 0),
-    ('mm', 9, 0, 2, 0),
-    ('mm', 9, 0, 3, 0),
-    ('mm', 9, 0, 4, 0),
-    ('out', 9, 0, 's', 0),
-    ('ilv', 11, 0, 's'),
-    ('ilv', 11, 1, 'v'),
-    ('mm', 9, 1, 0, 0),
-    ('mm', 9, 1, 1, 0),
-    ('mm', 9, 1, 2, 0),
-    ('mm', 9, 1, 3, 0),
-    ('mm', 9, 1, 4, 0),
-    ('out', 9, 1, 's', 0),
-    ('store', 9),
-    ('quant', (11, 0)),
-    ('quant', (11, 2)),
-    ('mm', 10, 0, 0, 0),
-    ('mm', 10, 0, 1, 0),
-    ('mm', 10, 0, 2, 0),
-    ('mm', 10, 0, 3, 0),
-    ('mm', 10, 0, 4, 0),
-    ('out', 10, 0, 's', 1),
-    ('mm', 10, 1, 0, 0),
-    ('mm', 10, 1, 1, 0),
-    ('mm', 10, 1, 2, 0),
-    ('mm', 10, 1, 3, 0),
-    ('mm', 10, 1, 4, 0),
-    ('out', 10, 1, 's', 1),
-    ('mm', 11, 0, 0, 0),
-    ('mm', 11, 0, 1, 0),
-    ('mm', 11, 0, 2, 0),
-    ('mm', 11, 0, 3, 0),
-    ('mm', 11, 0, 4, 0),
-    ('out', 11, 0, 's', 1),
-    ('mm', 11, 1, 0, 0),
-    ('mm', 11, 1, 1, 0),
-    ('mm', 11, 1, 2, 0),
-    ('mm', 11, 1, 3, 0),
-    ('mm', 11, 1, 4, 0),
-    ('out', 11, 1, 's', 2),
-]
+FIRST = range(3)
+ON_VECTOR = range(8, TILES)
+STORE_BY_HALF = 10
+
+PARTED_BUFS = 6
+GROUPED_BUFS = 6
+LOW_GROUPED_BUFS = 2
+FLIPPED_BUFS = 2
+
+
+def slabs_of(tiles, passes):
+    return [(i, c) for i in tiles for c in passes]
+
+
+def by_bank(slabs):
+    return [tuple(slabs[b:b + SLABS_PER_BANK]) for b in range(0, len(slabs), SLABS_PER_BANK)]
 
 
 def tile_stacked_rtrl_step_e4_kernel(tc, g_words, g_scales, w, u, low, h, out):
@@ -327,14 +53,14 @@ def tile_stacked_rtrl_step_e4_kernel(tc, g_words, g_scales, w, u, low, h, out):
     w_rows = w.rearrange("(i p) k -> p i k", p=P)
     u_rows = u.rearrange("(i p) k -> p i k", p=P)
     out_rows = out.rearrange("(i p) n -> p i n", p=P)
-    w_quarters = w.rearrange("m k -> (m k)").rearrange("(i r y q x) -> i q r y x", i=TILES, r=32, q=4, x=P)
+    w_quarters = w.rearrange("m k -> (m k)").rearrange("(i r y q x) -> i q r y x", i=TILES, r=QUAD, q=QUADS, x=P)
     g_bytes = g_words.rearrange("g p n t -> p g (n t)")
     g_scale_rows = g_scales.rearrange("g q n -> q g n")
 
     with ExitStack() as ctx:
         keep = ctx.enter_context(tc.tile_pool(name="keep", bufs=1))
-        work = ctx.enter_context(tc.tile_pool(name="work", bufs=4))
-        psum = ctx.enter_context(tc.psum_pool(name="psum", bufs=4))
+        work = ctx.enter_context(tc.tile_pool(name="work", bufs=1))
+        psum = ctx.enter_context(tc.psum_pool(name="psum", bufs=1))
         ctx.enter_context(tc.manual_schedule())
 
         ident = keep.tile([P, P], F32, name="ident")
@@ -347,165 +73,303 @@ def tile_stacked_rtrl_step_e4_kernel(tc, g_words, g_scales, w, u, low, h, out):
         slope_rows = keep.tile([P, P], F32, name="slope_rows")
         nc.scalar.activation(out=slope_rows[:], in_=ident[:], func=COPY, bias=0.0, scale=0.0)
 
-        g_plane = [keep.tile([P, W_PASSES, HALF], U8, name="g_plane%d" % hf, align_bytes=64) for hf in range(2)]
+        g_scale_sb = [keep.tile([P, W_PASSES, HALF], U8, name="g_scale%d" % hf, align_bytes=MX_ALIGN) for hf in range(2)]
         for hf in range(2):
-            nc.vector.memset(g_plane[hf][:].bitcast(I32), 0)
-        g_codes = [keep.tile([P, W_PASSES, HALF], U32, name="g_codes%d" % hf, align_bytes=64) for hf in range(2)]
+            nc.vector.memset(g_scale_sb[hf][:].bitcast(I32), 0)
+        g_codes = [keep.tile([P, W_PASSES, HALF], U32, name="g_codes%d" % hf, align_bytes=MX_ALIGN) for hf in range(2)]
         rows = [keep.tile([P, H + D], BF16, name="rows%d" % i, align_bytes=64) for i in range(TILES)]
-        low_raw, low_grouped, low_codes, low_plane = {}, {}, {}, {}
+        low_raw = {}
 
-        for item in LOADS:
-            if item[0] == "w":
-                nc.sync.dma_start(out=rows[item[1]][:, 0:H], in_=w_rows[:, item[1], :])
-            elif item[0] == "wq":
+        def load_w(i):
+            if i in ON_VECTOR:
                 for q in (0, 2, 1, 3):
-                    nc.sync.dma_start(out=rows[item[1]][32 * q:32 * q + 32, 0:H].rearrange("r (y x) -> r y x", x=P),
-                                      in_=w_quarters[item[1], q])
-            elif item[0] == "u":
-                nc.sync.dma_start(out=rows[item[1]][:, H:H + D], in_=u_rows[:, item[1], :])
-            elif item[0] == "gs":
-                hf = item[1]
-                for q in range(4):
-                    nc.sync.dma_start(out=g_plane[hf][32 * q:32 * q + 4, :, :].bitcast(I32),
-                                      in_=g_scale_rows[4 * q:4 * q + 4, :, hf * HALF:(hf + 1) * HALF].bitcast(I32))
-            elif item[0] == "g":
-                hf, c = item[1], item[2]
-                nc.sync.dma_start(out=g_codes[hf][:, c, :].bitcast(I32), in_=g_bytes[:, c, 4 * hf * HALF:4 * (hf + 1) * HALF].bitcast(I32))
+                    nc.sync.dma_start(out=rows[i][QUAD * q:QUAD * (q + 1), 0:H].rearrange("r (y x) -> r y x", x=P),
+                                      in_=w_quarters[i, q])
             else:
-                c, hf = item[1], item[2]
-                low_raw[c, hf] = keep.tile([P, 4, HALF], BF16, name="low_raw%d%d" % (c, hf), align_bytes=64)
-                nc.sync.dma_start(out=low_raw[c, hf][:],
-                                  in_=low[c * K_PASS:(c + 1) * K_PASS, hf * HALF:(hf + 1) * HALF].rearrange("(p t) n -> p t n", t=4))
+                nc.sync.dma_start(out=rows[i][:, 0:H], in_=w_rows[:, i, :])
+
+        def load_u(i):
+            nc.sync.dma_start(out=rows[i][:, H:H + D], in_=u_rows[:, i, :])
+
+        def load_g_scales(hf):
+            for q in range(QUADS):
+                nc.sync.dma_start(out=g_scale_sb[hf][QUAD * q:QUAD * q + 4, :, :].bitcast(I32),
+                                  in_=g_scale_rows[4 * q:4 * q + 4, :, hf * HALF:(hf + 1) * HALF].bitcast(I32))
+
+        def load_g(hf, c):
+            nc.sync.dma_start(out=g_codes[hf][:, c, :].bitcast(I32),
+                              in_=g_bytes[:, c, PACK * hf * HALF:PACK * (hf + 1) * HALF].bitcast(I32))
+
+        def load_low(hf, c):
+            k0 = (c - W_PASSES) * K_PASS
+            low_raw[hf, c] = keep.tile([P, PACK, HALF], BF16, name="low_raw%d%d" % (hf, c), align_bytes=64)
+            nc.sync.dma_start(out=low_raw[hf, c][:],
+                              in_=low[k0:k0 + K_PASS, hf * HALF:(hf + 1) * HALF].rearrange("(p t) n -> p t n", t=PACK))
+
+        for i in FIRST:
+            load_w(i)
+        for i in FIRST:
+            load_u(i)
+        load_low(0, 3)
+        load_g_scales(0)
+        load_g(0, 0)
+        load_g(0, 1)
+        load_low(0, 4)
+        load_g(0, 2)
+        load_g_scales(1)
+        load_g(1, 0)
+        load_w(3)
+        load_u(3)
+        load_g(1, 1)
+        load_g(1, 2)
+        load_low(1, 3)
+        load_w(4)
+        load_low(1, 4)
+        load_u(4)
+        for i in range(5, ON_VECTOR.start):
+            load_w(i)
+            load_u(i)
+        load_w(ON_VECTOR.start)
+        for i in ON_VECTOR:
+            load_u(i)
+        for i in range(ON_VECTOR.start + 1, TILES):
+            load_w(i)
 
         h_squared = keep.tile([TILES, P], F32, name="h_squared")
         slope = keep.tile([P, TILES], F32, name="slope")
 
-        free_banks = list(range(8))
-        held, done_passes, blocks, flipped, whole = {}, {}, {}, {}, {}
+        slab_codes = keep.tile([P, TILES * PASSES * P], U32, name="slab_codes", align_bytes=MX_ALIGN)
+        slab_scales = keep.tile([P, TILES * PASSES * P], U8, name="slab_scales", align_bytes=MX_ALIGN)
 
-        def take_bank(key, shape):
-            held[key] = free_banks.pop(0)
-            return psum.tile(shape, F32, name="bank%d" % held[key], tag="bank%d" % held[key], bufs=1)
+        free_banks = list(range(BANKS))
+        held = {}
 
-        sources, banks, groups, codes, planes, sums = {}, {}, {}, {}, {}, {}
+        def take_bank(user, shape):
+            number = free_banks.pop(0)
+            bank = psum.tile(shape, F32, name="bank%d" % number, tag="bank%d" % number)
+            held[user] = (number, bank)
+            return bank
 
-        def copy_on(engine, dst, src):
-            if engine == "v":
-                nc.vector.tensor_copy(out=dst, in_=src)
-            else:
-                nc.scalar.copy(out=dst, in_=src)
+        def give_back(user):
+            number, bank = held[user]
+            free_banks.append(number)
+            return bank
 
-        def pairs_of(i, c0, c1):
-            return rows[i][:].bitcast(F32)[:, c0 * PAIRS:c1 * PAIRS].rearrange("p (j e) -> p e j", e=2)
+        parted, flipped, grouped, low_grouped, stationary, moving, passes_done, results = {}, {}, {}, {}, {}, {}, {}, {}
+        for hf in range(2):
+            for c in range(W_PASSES):
+                moving[hf, c] = (g_codes[hf][:, c, :].bitcast(E5M2), g_scale_sb[hf][:, c, :])
+        on_vector, on_scalar = nc.vector.tensor_copy, nc.scalar.copy
 
-        for step in STEPS:
-            kind = step[0]
-            if kind == "weave":
-                c, hf, n0, n1, engine = step[1:]
-                if (c, hf) not in low_grouped:
-                    low_grouped[c, hf] = work.tile([P, HALF, 4], BF16, name="low_grouped", tag="low_grouped", bufs=2, align_bytes=64)
-                copy_on(engine, low_grouped[c, hf][:, n0:n1, :].rearrange("p (a b) t -> p a t b", b=4),
-                        low_raw[c, hf][:, :, n0:n1].rearrange("p t (a b) -> p a t b", b=4))
-            elif kind == "lowq":
-                c, hf = step[1:]
-                low_codes[c, hf] = keep.tile([P, HALF], U32, name="low_codes%d%d" % (c, hf), align_bytes=64)
-                low_plane[c, hf] = keep.tile([P, HALF], U8, name="low_plane%d%d" % (c, hf), align_bytes=64)
-                nc.vector.quantize_mx(out=low_codes[c, hf][:].bitcast(E4M3), scales=low_plane[c, hf][:],
-                                      in_=low_grouped[c, hf][:].rearrange("p n t -> p (n t)"))
-            elif kind == "split":
-                i, c0, c1, engine = step[1:]
-                if engine == "n":
-                    continue
-                split = work.tile([P, 2, (c1 - c0) * P], F32, name="split", tag="split", bufs=6, align_bytes=64)
-                if ("wq", i) in LOADS and c0 == 0:
-                    copy_on(engine, split[:].rearrange("p e (b x) -> p (e b x)", b=4).rearrange("p (b e x) -> p b e x", b=4, e=2),
-                            rows[i][:].bitcast(F32)[:, 0:H // 2].rearrange("p (b x e) -> p b e x", b=4, e=2))
-                    blocks[i] = split
-                    continue
-                copy_on(engine, split[:], pairs_of(i, c0, c1))
-                for c in range(c0, c1):
-                    sources[i, c] = split[:, :, (c - c0) * P:(c - c0 + 1) * P]
-            elif kind == "slope_rows":
-                nc.scalar.activation(out=h_squared[:], in_=h_sb[:], func=SQUARE)
-                nc.scalar.activation(out=slope_rows[0:TILES, :], in_=h_squared[:], func=COPY, bias=1.0, scale=-1.0)
-            elif kind == "slope_turn":
-                slope_bank = take_bank("slope", [P, P])
-                nc.tensor.transpose(out=slope_bank[:], in_=slope_rows[:], identity=ident[:])
-            elif kind == "slope_out":
-                free_banks.append(held["slope"])
-                nc.scalar.copy(out=slope[:], in_=slope_bank[:, 0:TILES])
-            elif kind == "dvt":
-                i = step[1]
-                flipped[i] = work.tile([P, H // 2], F32, name="flipped", tag="flipped", bufs=2, align_bytes=64)
-                nc.vector.transpose(out=flipped[i][:], in_=blocks[i][:].rearrange("p e x -> p (e x)"))
-            elif kind == "ilv":
-                i, part, engine = step[1:]
-                units = ((i, 0), (i, 1)) if part == 0 else ((i, 2),)
-                banks[units[0]] = (units, None)
-                groups[units[0]] = work.tile([P, len(units) * K_PASS], BF16, name="grouped", tag="grouped", bufs=6, align_bytes=64)
-                dst = groups[units[0]][:].bitcast(F32).rearrange("p (c r a y) -> p a c r y", r=32, a=2, y=4)
-                src = flipped[i][:].rearrange("p (a y c r) -> p a c r y", a=2, y=4, r=32)
-                for a in range(2):
-                    copy_on(engine, dst[:, a], src[:, a, units[0][1]:units[-1][1] + 1])
-            elif kind == "store":
-                nc.sync.dma_start(out=out_rows[:, step[1], :], in_=whole[step[1]][:])
-            elif kind == "turn":
-                units = step[1]
-                bank = take_bank(("turned", units[0]), [P, len(units), 2, P])
-                for s, (i, c) in enumerate(units):
-                    source = sources[i, c] if (i, c) in sources else pairs_of(i, c, c + 1)
-                    for e in range(2):
-                        nc.tensor.transpose(out=bank[:, s, e, :], in_=source[:, e, :], identity=ident[:])
-                banks[units[0]] = (units, bank)
-            elif kind == "empty":
-                first, engine = step[1:]
-                units, bank = banks[first]
-                free_banks.append(held["turned", first])
-                groups[first] = work.tile([P, len(units) * K_PASS], BF16, name="grouped", tag="grouped", bufs=6, align_bytes=64)
-                copy_on(engine, groups[first][:].bitcast(F32).rearrange("p (s m e) -> p s m e", m=P, e=2),
-                        bank[:].rearrange("p s e m -> p s m e"))
-            elif kind == "quant":
-                first = step[1]
-                units = banks[first][0]
-                unit_codes = keep.tile([P, len(units) * P], U32, name="codes%d_%d" % first, align_bytes=64)
-                unit_plane = keep.tile([P, len(units) * P], U8, name="plane%d_%d" % first, align_bytes=64)
-                nc.vector.quantize_mx(out=unit_codes[:].bitcast(E4M3), scales=unit_plane[:], in_=groups[first][:])
-                for s, unit in enumerate(units):
-                    codes[unit] = unit_codes[:, s * P:(s + 1) * P]
-                    planes[unit] = unit_plane[:, s * P:(s + 1) * P]
-                if first == (0, 0):
-                    warm_codes, warm_plane = unit_codes, unit_plane
-            elif kind == "warm":
-                scratch = take_bank("warm", [P, 2 * P])
-                free_banks.append(held["warm"])
-                for repeat in range(step[1]):
-                    nc.tensor.matmul_mx(out=scratch[:], lhsT=codes[0, 0].bitcast(E4M3), lhsT_scale=planes[0, 0],
-                                        rhs=warm_codes[:].bitcast(E4M3), rhs_scale=warm_plane[:], start=True, stop=True)
-            elif kind == "mm":
-                i, hf, c = step[1:4]
-                before = done_passes.get((i, hf), 0)
-                done_passes[i, hf] = before + 1
-                if before == 0:
-                    sums[i, hf] = take_bank(("sums", i, hf), [P, HALF])
-                if c < W_PASSES:
-                    moving, moving_plane = g_codes[hf][:, c, :].bitcast(E5M2), g_plane[hf][:, c, :]
-                else:
-                    moving, moving_plane = low_codes[c - W_PASSES, hf][:].bitcast(E4M3), low_plane[c - W_PASSES, hf][:]
-                nc.tensor.matmul_mx(out=sums[i, hf][:], lhsT=codes[i, c].bitcast(E4M3), lhsT_scale=planes[i, c],
-                                    rhs=moving, rhs_scale=moving_plane, start=(before == 0), stop=(before == PASSES - 1))
-            else:
-                i, hf, engine, pieces = step[1:]
-                free_banks.append(held["sums", i, hf])
-                if i not in whole:
-                    whole[i] = keep.tile([P, N], F32, name="result%d" % i)
-                result = whole[i][:, hf * HALF:(hf + 1) * HALF]
-                store_now = pieces > 0
-                pieces = max(pieces, 1)
-                for n0 in range(0, HALF, HALF // pieces):
-                    cols = slice(n0, n0 + HALF // pieces)
-                    if engine == "v":
-                        nc.vector.tensor_scalar(out=result[:, cols], in0=sums[i, hf][:, cols], scalar1=slope[:, i:i + 1], scalar2=None, op0=MULT)
-                    else:
-                        nc.scalar.activation(out=result[:, cols], in_=sums[i, hf][:, cols], func=COPY, scale=slope[:, i:i + 1])
-                    if store_now:
-                        nc.sync.dma_start(out=out_rows[:, i, hf * HALF + n0:hf * HALF + n0 + HALF // pieces], in_=result[:, cols])
+        def part(i, first, last):
+            tile = work.tile([P, 2, (last - first) * P], F32, name="parted", tag="parted", bufs=PARTED_BUFS, align_bytes=MX_ALIGN)
+            pairs = rows[i][:].bitcast(F32)[:, first * PAIRS:last * PAIRS]
+            nc.vector.tensor_copy(out=tile[:], in_=pairs.rearrange("p (j e) -> p e j", e=2))
+            for c in range(first, last):
+                parted[i, c] = tile[:, :, (c - first) * P:(c - first + 1) * P]
+
+        def part_w(i):
+            part(i, 0, W_PASSES)
+
+        def part_u(i):
+            part(i, W_PASSES, PASSES)
+
+        def turn(slabs):
+            bank = take_bank(slabs, [P, len(slabs), 2, P])
+            for s, slab in enumerate(slabs):
+                for e in range(2):
+                    nc.tensor.transpose(out=bank[:, s, e, :], in_=parted[slab][:, e, :], identity=ident[:])
+
+        def new_grouped(slabs):
+            grouped[slabs] = work.tile([P, len(slabs) * K_PASS], BF16, name="grouped", tag="grouped", bufs=GROUPED_BUFS,
+                                       align_bytes=MX_ALIGN)
+            return grouped[slabs][:].bitcast(F32)
+
+        def empty(slabs, copy):
+            bank = give_back(slabs)
+            copy(out=new_grouped(slabs).rearrange("p (s m e) -> p s m e", m=P, e=2), in_=bank[:].rearrange("p s e m -> p s m e"))
+
+        def quantise(slabs):
+            cols = slice(len(stationary) * P, (len(stationary) + len(slabs)) * P)
+            codes, scales = slab_codes[:, cols], slab_scales[:, cols]
+            nc.vector.quantize_mx(out=codes.bitcast(E4M3), scales=scales, in_=grouped[slabs][:])
+            for s, slab in enumerate(slabs):
+                stationary[slab] = (codes[:, s * P:(s + 1) * P].bitcast(E4M3), scales[:, s * P:(s + 1) * P])
+
+        def turn_run(slabs):
+            banks = by_bank(slabs)
+            for bank_slabs in banks:
+                turn(bank_slabs)
+            return banks
+
+        def part_quarters(i):
+            tile = work.tile([P, 2, W_PASSES * P], F32, name="parted", tag="parted", bufs=PARTED_BUFS, align_bytes=MX_ALIGN)
+            parted[i] = tile[:].rearrange("p e x -> p (e x)")
+            nc.vector.tensor_copy(out=parted[i].rearrange("p (b e x) -> p b e x", b=4, e=2),
+                                  in_=rows[i][:].bitcast(F32)[:, 0:H // 2].rearrange("p (b x e) -> p b e x", b=4, e=2))
+
+        def flip(i):
+            flipped[i] = work.tile([P, H // 2], F32, name="flipped", tag="flipped", bufs=FLIPPED_BUFS, align_bytes=MX_ALIGN)
+            nc.vector.transpose(out=flipped[i][:], in_=parted[i])
+
+        def gather(slabs, copy):
+            i, first = slabs[0]
+            dst = new_grouped(slabs).rearrange("p (c r a y) -> p a c r y", r=QUAD, a=2, y=4)
+            src = flipped[i][:].rearrange("p (a y c r) -> p a c r y", a=2, y=4, r=QUAD)
+            for a in range(2):
+                copy(out=dst[:, a], in_=src[:, a, first:first + len(slabs)])
+
+        def interleave_low(hf, c):
+            low_grouped[hf, c] = work.tile([P, HALF, PACK], BF16, name="low_grouped", tag="low_grouped",
+                                           bufs=LOW_GROUPED_BUFS, align_bytes=MX_ALIGN)
+            for cols, copy in ((slice(0, HALF // 2), on_vector), (slice(HALF // 2, HALF), on_scalar)):
+                copy(out=low_grouped[hf, c][:, cols, :].rearrange("p (a b) t -> p a t b", b=4),
+                     in_=low_raw[hf, c][:, :, cols].rearrange("p t (a b) -> p a t b", b=4))
+
+        def quantise_low(hf, c):
+            codes = keep.tile([P, HALF], U32, name="low_codes%d%d" % (hf, c), align_bytes=MX_ALIGN)
+            scales = keep.tile([P, HALF], U8, name="low_scales%d%d" % (hf, c), align_bytes=MX_ALIGN)
+            nc.vector.quantize_mx(out=codes[:].bitcast(E4M3), scales=scales[:],
+                                  in_=low_grouped[hf, c][:].rearrange("p n t -> p (n t)"))
+            moving[hf, c] = (codes[:].bitcast(E4M3), scales[:])
+
+        def multiply(tiles, hf, passes):
+            for c in passes:
+                for i in tiles:
+                    before = passes_done.get((i, hf), 0)
+                    passes_done[i, hf] = before + 1
+                    if before == 0:
+                        take_bank((i, hf), [P, HALF])
+                    nc.tensor.matmul_mx(out=held[i, hf][1][:], lhsT=stationary[i, c][0], lhsT_scale=stationary[i, c][1],
+                                        rhs=moving[hf, c][0], rhs_scale=moving[hf, c][1],
+                                        start=(before == 0), stop=(before == PASSES - 1))
+
+        def finish(i, hf):
+            bank = give_back((i, hf))
+            if hf == 0:
+                results[i] = keep.tile([P, N], F32, name="result%d" % i)
+            width = HALF // 2 if (i, hf) == (TILES - 1, 1) else HALF
+            for n0 in range(0, HALF, width):
+                cols = slice(hf * HALF + n0, hf * HALF + n0 + width)
+                nc.scalar.activation(out=results[i][:, cols], in_=bank[:, n0:n0 + width], func=COPY, scale=slope[:, i:i + 1])
+                if i >= STORE_BY_HALF:
+                    nc.sync.dma_start(out=out_rows[:, i, cols], in_=results[i][:, cols])
+            if i < STORE_BY_HALF and hf == 1:
+                nc.sync.dma_start(out=out_rows[:, i, :], in_=results[i][:])
+
+        w_passes, u_passes, all_passes = range(W_PASSES), range(W_PASSES, PASSES), range(PASSES)
+
+        banks = by_bank(slabs_of(FIRST, w_passes) + slabs_of(FIRST, u_passes))
+        part_w(0)
+        part_w(1)
+        nc.scalar.activation(out=h_squared[:], in_=h_sb[:], func=SQUARE)
+        nc.scalar.activation(out=slope_rows[0:TILES, :], in_=h_squared[:], func=COPY, bias=1.0, scale=-1.0)
+        part_w(2)
+        for b in range(4):
+            turn(banks[b])
+        empty(banks[0], on_scalar)
+        empty(banks[1], on_scalar)
+        part_u(0)
+        quantise(banks[0])
+        part_u(1)
+        quantise(banks[1])
+        part_u(2)
+        for b in range(4, BANKS):
+            turn(banks[b])
+        nc.tensor.transpose(out=take_bank("slope", [P, P])[:], in_=slope_rows[:], identity=ident[:])
+        for b in range(2, 5):
+            empty(banks[b], on_scalar)
+        quantise(banks[2])
+        quantise(banks[3])
+        interleave_low(0, 3)
+        quantise(banks[4])
+        empty(banks[5], on_scalar)
+        empty(banks[6], on_vector)
+        quantise_low(0, 3)
+        nc.scalar.copy(out=slope[:], in_=give_back("slope")[:, 0:TILES])
+        empty(banks[7], on_scalar)
+        quantise(banks[5])
+        quantise(banks[6])
+
+        multiply(FIRST, 0, [0, 1])
+        interleave_low(0, 4)
+        quantise(banks[7])
+        quantise_low(0, 4)
+        multiply(FIRST, 0, [3, 2])
+        multiply(FIRST, 1, [0])
+        part_w(3)
+        part_u(3)
+        multiply([0], 0, [4])
+        finish(0, 0)
+        multiply([1], 0, [4])
+        finish(1, 0)
+        multiply([2], 0, [4])
+        banks = turn_run(slabs_of([3], all_passes))
+        for bank_slabs, copy in zip(banks, (on_vector, on_scalar, on_vector)):
+            empty(bank_slabs, copy)
+        for bank_slabs in banks:
+            quantise(bank_slabs)
+        finish(2, 0)
+        multiply(FIRST, 1, [1, 2])
+        interleave_low(1, 3)
+        part_w(4)
+        quantise_low(1, 3)
+        multiply([3], 0, all_passes)
+        multiply([3], 1, w_passes)
+        interleave_low(1, 4)
+        finish(3, 0)
+        part_u(4)
+        quantise_low(1, 4)
+        multiply(range(4), 1, [3])
+        banks = turn_run(slabs_of([4], all_passes))
+        for bank_slabs, copy in zip(banks, (on_scalar, on_scalar, on_vector)):
+            empty(bank_slabs, copy)
+        for bank_slabs in banks:
+            quantise(bank_slabs)
+        for i in FIRST:
+            multiply([i], 1, [4])
+            finish(i, 1)
+        multiply([3], 1, [4])
+        part_w(5)
+        finish(3, 1)
+
+        part_u(5)
+        for i in range(6, ON_VECTOR.start):
+            part_w(i)
+            part_u(i)
+        multiply([4], 0, all_passes)
+        finish(4, 0)
+        banks = turn_run(slabs_of(range(5, ON_VECTOR.start), all_passes))
+        for b, bank_slabs in enumerate(banks):
+            empty(bank_slabs, on_vector if b % 3 == 2 else on_scalar)
+        for bank_slabs in banks:
+            quantise(bank_slabs)
+        multiply([4], 1, all_passes)
+        finish(4, 1)
+
+        run_before = ON_VECTOR.start - 1
+        for i in range(5, TILES):
+            if i == run_before:
+                banks = turn_run(slabs_of(ON_VECTOR, u_passes))
+            if i + 2 in ON_VECTOR:
+                part_quarters(i + 2)
+            if i + 1 in ON_VECTOR:
+                for bank_slabs in by_bank(slabs_of([i + 1], w_passes)):
+                    quantise(bank_slabs)
+            if i + 2 in ON_VECTOR:
+                flip(i + 2)
+            if i == run_before:
+                for bank_slabs in banks:
+                    empty(bank_slabs, on_scalar)
+                for bank_slabs in banks:
+                    quantise(bank_slabs)
+            if i + 1 == run_before:
+                for later in ON_VECTOR:
+                    part_u(later)
+            multiply([i], 0, all_passes)
+            finish(i, 0)
+            if i + 2 in ON_VECTOR:
+                for bank_slabs, copy in zip(by_bank(slabs_of([i + 2], w_passes)), (on_scalar, on_vector)):
+                    gather(bank_slabs, copy)
+            multiply([i], 1, all_passes)
+            finish(i, 1)

from contextlib import ExitStack

import concourse.mybir as mybir
from concourse.masks import make_identity

H, D, N = 1536, 1024, 1024
FLOPS = 2 * H * N * (H + D)

F32 = mybir.dt.float32
BF16 = mybir.dt.bfloat16
I32 = mybir.dt.int32
U32 = mybir.dt.uint32
U8 = mybir.dt.uint8
E4M3 = mybir.dt.float8_e4m3fn_x4
E5M2 = mybir.dt.float8_e5m2_x4
COPY = mybir.ActivationFunctionType.Copy
SQUARE = mybir.ActivationFunctionType.Square

P = 128
QUAD = 32
QUADS = P // QUAD
PACK = 4
K_PASS = P * PACK
PAIRS = K_PASS // 2
HALF = 512
TILES = H // P
W_PASSES = H // K_PASS
PASSES = W_PASSES + D // K_PASS
BANKS = 8
SLABS_PER_BANK = 2
MX_ALIGN = 256

FIRST = range(3)
ON_VECTOR = range(8, TILES)
STORE_BY_HALF = 10

PARTED_BUFS = 6
GROUPED_BUFS = 6
LOW_GROUPED_BUFS = 2
FLIPPED_BUFS = 2


def slabs_of(tiles, passes):
    return [(i, c) for i in tiles for c in passes]


def by_bank(slabs):
    return [tuple(slabs[b:b + SLABS_PER_BANK]) for b in range(0, len(slabs), SLABS_PER_BANK)]


def tile_stacked_rtrl_step_e4_kernel(tc, g_words, g_scales, w, u, low, h, out):
    nc = tc.nc
    w_rows = w.rearrange("(i p) k -> p i k", p=P)
    u_rows = u.rearrange("(i p) k -> p i k", p=P)
    out_rows = out.rearrange("(i p) n -> p i n", p=P)
    w_quarters = w.rearrange("m k -> (m k)").rearrange("(i r y q x) -> i q r y x", i=TILES, r=QUAD, q=QUADS, x=P)
    g_bytes = g_words.rearrange("g p n t -> p g (n t)")
    g_scale_rows = g_scales.rearrange("g q n -> q g n")

    with ExitStack() as ctx:
        keep = ctx.enter_context(tc.tile_pool(name="keep", bufs=1))
        work = ctx.enter_context(tc.tile_pool(name="work", bufs=1))
        psum = ctx.enter_context(tc.psum_pool(name="psum", bufs=1))
        ctx.enter_context(tc.manual_schedule())

        ident = keep.tile([P, P], F32, name="ident")
        make_identity(nc, ident[:])

        h_sb = keep.tile([TILES, P], BF16, name="h_sb")
        h_rows = h.rearrange("(i p) -> i p", p=P)
        nc.scalar.dma_start(out=h_sb[0:8, :], in_=h_rows[0:8, :])
        nc.scalar.dma_start(out=h_sb[8:TILES, :], in_=h_rows[8:TILES, :])
        slope_rows = keep.tile([P, P], F32, name="slope_rows")
        nc.scalar.activation(out=slope_rows[:], in_=ident[:], func=COPY, bias=0.0, scale=0.0)

        g_scale_sb = [keep.tile([P, W_PASSES, HALF], U8, name="g_scale%d" % hf, align_bytes=MX_ALIGN) for hf in range(2)]
        for hf in range(2):
            nc.vector.memset(g_scale_sb[hf][:].bitcast(I32), 0)
        g_codes = [keep.tile([P, W_PASSES, HALF], U32, name="g_codes%d" % hf, align_bytes=MX_ALIGN) for hf in range(2)]
        rows = [keep.tile([P, H + D], BF16, name="rows%d" % i, align_bytes=64) for i in range(TILES)]
        low_raw = {}

        def load_w(i):
            if i in ON_VECTOR:
                for q in (0, 2, 1, 3):
                    nc.sync.dma_start(out=rows[i][QUAD * q:QUAD * (q + 1), 0:H].rearrange("r (y x) -> r y x", x=P),
                                      in_=w_quarters[i, q])
            else:
                nc.sync.dma_start(out=rows[i][:, 0:H], in_=w_rows[:, i, :])

        def load_u(i):
            nc.sync.dma_start(out=rows[i][:, H:H + D], in_=u_rows[:, i, :])

        def load_g_scales(hf):
            for q in range(QUADS):
                nc.sync.dma_start(out=g_scale_sb[hf][QUAD * q:QUAD * q + 4, :, :].bitcast(I32),
                                  in_=g_scale_rows[4 * q:4 * q + 4, :, hf * HALF:(hf + 1) * HALF].bitcast(I32))

        def load_g(hf, c):
            nc.sync.dma_start(out=g_codes[hf][:, c, :].bitcast(I32),
                              in_=g_bytes[:, c, PACK * hf * HALF:PACK * (hf + 1) * HALF].bitcast(I32))

        def load_low(hf, c):
            k0 = (c - W_PASSES) * K_PASS
            low_raw[hf, c] = keep.tile([P, PACK, HALF], BF16, name="low_raw%d%d" % (hf, c), align_bytes=64)
            nc.sync.dma_start(out=low_raw[hf, c][:],
                              in_=low[k0:k0 + K_PASS, hf * HALF:(hf + 1) * HALF].rearrange("(p t) n -> p t n", t=PACK))

        for i in FIRST:
            load_w(i)
        for i in FIRST:
            load_u(i)
        load_low(0, 3)
        load_g_scales(0)
        load_g(0, 0)
        load_g(0, 1)
        load_low(0, 4)
        load_g(0, 2)
        load_g_scales(1)
        load_g(1, 0)
        load_w(3)
        load_u(3)
        load_g(1, 1)
        load_g(1, 2)
        load_low(1, 3)
        load_w(4)
        load_low(1, 4)
        load_u(4)
        for i in range(5, ON_VECTOR.start):
            load_w(i)
            load_u(i)
        load_w(ON_VECTOR.start)
        for i in ON_VECTOR:
            load_u(i)
        for i in range(ON_VECTOR.start + 1, TILES):
            load_w(i)

        h_squared = keep.tile([TILES, P], F32, name="h_squared")
        slope = keep.tile([P, TILES], F32, name="slope")

        slab_codes = keep.tile([P, TILES * PASSES * P], U32, name="slab_codes", align_bytes=MX_ALIGN)
        slab_scales = keep.tile([P, TILES * PASSES * P], U8, name="slab_scales", align_bytes=MX_ALIGN)

        free_banks = list(range(BANKS))
        held = {}

        def take_bank(user, shape):
            number = free_banks.pop(0)
            bank = psum.tile(shape, F32, name="bank%d" % number, tag="bank%d" % number)
            held[user] = (number, bank)
            return bank

        def give_back(user):
            number, bank = held[user]
            free_banks.append(number)
            return bank

        parted, flipped, grouped, low_grouped, stationary, moving, passes_done, results = {}, {}, {}, {}, {}, {}, {}, {}
        for hf in range(2):
            for c in range(W_PASSES):
                moving[hf, c] = (g_codes[hf][:, c, :].bitcast(E5M2), g_scale_sb[hf][:, c, :])
        on_vector, on_scalar = nc.vector.tensor_copy, nc.scalar.copy

        def part(i, first, last):
            tile = work.tile([P, 2, (last - first) * P], F32, name="parted", tag="parted", bufs=PARTED_BUFS, align_bytes=MX_ALIGN)
            pairs = rows[i][:].bitcast(F32)[:, first * PAIRS:last * PAIRS]
            nc.vector.tensor_copy(out=tile[:], in_=pairs.rearrange("p (j e) -> p e j", e=2))
            for c in range(first, last):
                parted[i, c] = tile[:, :, (c - first) * P:(c - first + 1) * P]

        def part_w(i):
            part(i, 0, W_PASSES)

        def part_u(i):
            part(i, W_PASSES, PASSES)

        def turn(slabs):
            bank = take_bank(slabs, [P, len(slabs), 2, P])
            for s, slab in enumerate(slabs):
                for e in range(2):
                    nc.tensor.transpose(out=bank[:, s, e, :], in_=parted[slab][:, e, :], identity=ident[:])

        def new_grouped(slabs):
            grouped[slabs] = work.tile([P, len(slabs) * K_PASS], BF16, name="grouped", tag="grouped", bufs=GROUPED_BUFS,
                                       align_bytes=MX_ALIGN)
            return grouped[slabs][:].bitcast(F32)

        def empty(slabs, copy):
            bank = give_back(slabs)
            copy(out=new_grouped(slabs).rearrange("p (s m e) -> p s m e", m=P, e=2), in_=bank[:].rearrange("p s e m -> p s m e"))

        def quantise(slabs):
            cols = slice(len(stationary) * P, (len(stationary) + len(slabs)) * P)
            codes, scales = slab_codes[:, cols], slab_scales[:, cols]
            nc.vector.quantize_mx(out=codes.bitcast(E4M3), scales=scales, in_=grouped[slabs][:])
            for s, slab in enumerate(slabs):
                stationary[slab] = (codes[:, s * P:(s + 1) * P].bitcast(E4M3), scales[:, s * P:(s + 1) * P])

        def turn_run(slabs):
            banks = by_bank(slabs)
            for bank_slabs in banks:
                turn(bank_slabs)
            return banks

        def part_quarters(i):
            tile = work.tile([P, 2, W_PASSES * P], F32, name="parted", tag="parted", bufs=PARTED_BUFS, align_bytes=MX_ALIGN)
            parted[i] = tile[:].rearrange("p e x -> p (e x)")
            nc.vector.tensor_copy(out=parted[i].rearrange("p (b e x) -> p b e x", b=4, e=2),
                                  in_=rows[i][:].bitcast(F32)[:, 0:H // 2].rearrange("p (b x e) -> p b e x", b=4, e=2))

        def flip(i):
            flipped[i] = work.tile([P, H // 2], F32, name="flipped", tag="flipped", bufs=FLIPPED_BUFS, align_bytes=MX_ALIGN)
            nc.vector.transpose(out=flipped[i][:], in_=parted[i])

        def gather(slabs, copy):
            i, first = slabs[0]
            dst = new_grouped(slabs).rearrange("p (c r a y) -> p a c r y", r=QUAD, a=2, y=4)
            src = flipped[i][:].rearrange("p (a y c r) -> p a c r y", a=2, y=4, r=QUAD)
            for a in range(2):
                copy(out=dst[:, a], in_=src[:, a, first:first + len(slabs)])

        def interleave_low(hf, c):
            low_grouped[hf, c] = work.tile([P, HALF, PACK], BF16, name="low_grouped", tag="low_grouped",
                                           bufs=LOW_GROUPED_BUFS, align_bytes=MX_ALIGN)
            for cols, copy in ((slice(0, HALF // 2), on_vector), (slice(HALF // 2, HALF), on_scalar)):
                copy(out=low_grouped[hf, c][:, cols, :].rearrange("p (a b) t -> p a t b", b=4),
                     in_=low_raw[hf, c][:, :, cols].rearrange("p t (a b) -> p a t b", b=4))

        def quantise_low(hf, c):
            codes = keep.tile([P, HALF], U32, name="low_codes%d%d" % (hf, c), align_bytes=MX_ALIGN)
            scales = keep.tile([P, HALF], U8, name="low_scales%d%d" % (hf, c), align_bytes=MX_ALIGN)
            nc.vector.quantize_mx(out=codes[:].bitcast(E4M3), scales=scales[:],
                                  in_=low_grouped[hf, c][:].rearrange("p n t -> p (n t)"))
            moving[hf, c] = (codes[:].bitcast(E4M3), scales[:])

        def multiply(tiles, hf, passes):
            for c in passes:
                for i in tiles:
                    before = passes_done.get((i, hf), 0)
                    passes_done[i, hf] = before + 1
                    if before == 0:
                        take_bank((i, hf), [P, HALF])
                    nc.tensor.matmul_mx(out=held[i, hf][1][:], lhsT=stationary[i, c][0], lhsT_scale=stationary[i, c][1],
                                        rhs=moving[hf, c][0], rhs_scale=moving[hf, c][1],
                                        start=(before == 0), stop=(before == PASSES - 1))

        def finish(i, hf):
            bank = give_back((i, hf))
            if hf == 0:
                results[i] = keep.tile([P, N], F32, name="result%d" % i)
            width = HALF // 2 if (i, hf) == (TILES - 1, 1) else HALF
            for n0 in range(0, HALF, width):
                cols = slice(hf * HALF + n0, hf * HALF + n0 + width)
                nc.scalar.activation(out=results[i][:, cols], in_=bank[:, n0:n0 + width], func=COPY, scale=slope[:, i:i + 1])
                if i >= STORE_BY_HALF:
                    nc.sync.dma_start(out=out_rows[:, i, cols], in_=results[i][:, cols])
            if i < STORE_BY_HALF and hf == 1:
                nc.sync.dma_start(out=out_rows[:, i, :], in_=results[i][:])

        w_passes, u_passes, all_passes = range(W_PASSES), range(W_PASSES, PASSES), range(PASSES)

        banks = by_bank(slabs_of(FIRST, w_passes) + slabs_of(FIRST, u_passes))
        part_w(0)
        part_w(1)
        nc.scalar.activation(out=h_squared[:], in_=h_sb[:], func=SQUARE)
        nc.scalar.activation(out=slope_rows[0:TILES, :], in_=h_squared[:], func=COPY, bias=1.0, scale=-1.0)
        part_w(2)
        for b in range(4):
            turn(banks[b])
        empty(banks[0], on_scalar)
        empty(banks[1], on_scalar)
        part_u(0)
        quantise(banks[0])
        part_u(1)
        quantise(banks[1])
        part_u(2)
        for b in range(4, BANKS):
            turn(banks[b])
        nc.tensor.transpose(out=take_bank("slope", [P, P])[:], in_=slope_rows[:], identity=ident[:])
        for b in range(2, 5):
            empty(banks[b], on_scalar)
        quantise(banks[2])
        quantise(banks[3])
        interleave_low(0, 3)
        quantise(banks[4])
        empty(banks[5], on_scalar)
        empty(banks[6], on_vector)
        quantise_low(0, 3)
        nc.scalar.copy(out=slope[:], in_=give_back("slope")[:, 0:TILES])
        empty(banks[7], on_scalar)
        quantise(banks[5])
        quantise(banks[6])

        multiply(FIRST, 0, [0, 1])
        interleave_low(0, 4)
        quantise(banks[7])
        quantise_low(0, 4)
        multiply(FIRST, 0, [3, 2])
        multiply(FIRST, 1, [0])
        part_w(3)
        part_u(3)
        multiply([0], 0, [4])
        finish(0, 0)
        multiply([1], 0, [4])
        finish(1, 0)
        multiply([2], 0, [4])
        banks = turn_run(slabs_of([3], all_passes))
        for bank_slabs, copy in zip(banks, (on_vector, on_scalar, on_vector)):
            empty(bank_slabs, copy)
        for bank_slabs in banks:
            quantise(bank_slabs)
        finish(2, 0)
        multiply(FIRST, 1, [1, 2])
        interleave_low(1, 3)
        part_w(4)
        quantise_low(1, 3)
        multiply([3], 0, all_passes)
        multiply([3], 1, w_passes)
        interleave_low(1, 4)
        finish(3, 0)
        part_u(4)
        quantise_low(1, 4)
        multiply(range(4), 1, [3])
        banks = turn_run(slabs_of([4], all_passes))
        for bank_slabs, copy in zip(banks, (on_scalar, on_scalar, on_vector)):
            empty(bank_slabs, copy)
        for bank_slabs in banks:
            quantise(bank_slabs)
        for i in FIRST:
            multiply([i], 1, [4])
            finish(i, 1)
        multiply([3], 1, [4])
        part_w(5)
        finish(3, 1)

        part_u(5)
        for i in range(6, ON_VECTOR.start):
            part_w(i)
            part_u(i)
        multiply([4], 0, all_passes)
        finish(4, 0)
        banks = turn_run(slabs_of(range(5, ON_VECTOR.start), all_passes))
        for b, bank_slabs in enumerate(banks):
            empty(bank_slabs, on_vector if b % 3 == 2 else on_scalar)
        for bank_slabs in banks:
            quantise(bank_slabs)
        multiply([4], 1, all_passes)
        finish(4, 1)

        run_before = ON_VECTOR.start - 1
        for i in range(5, TILES):
            if i == run_before:
                banks = turn_run(slabs_of(ON_VECTOR, u_passes))
            if i + 2 in ON_VECTOR:
                part_quarters(i + 2)
            if i + 1 in ON_VECTOR:
                for bank_slabs in by_bank(slabs_of([i + 1], w_passes)):
                    quantise(bank_slabs)
            if i + 2 in ON_VECTOR:
                flip(i + 2)
            if i == run_before:
                for bank_slabs in banks:
                    empty(bank_slabs, on_scalar)
                for bank_slabs in banks:
                    quantise(bank_slabs)
            if i + 1 == run_before:
                for later in ON_VECTOR:
                    part_u(later)
            multiply([i], 0, all_passes)
            finish(i, 0)
            if i + 2 in ON_VECTOR:
                for bank_slabs, copy in zip(by_bank(slabs_of([i + 2], w_passes)), (on_scalar, on_vector)):
                    gather(bank_slabs, copy)
            multiply([i], 1, all_passes)
            finish(i, 1)
